import numpy as np
import ml_dtypes


def mxq(x, axis, fmt="e4m3"):
    dtype, down = {"e4m3": (ml_dtypes.float8_e4m3fn, 7), "e5m2": (ml_dtypes.float8_e5m2, 14)}[fmt]
    v = np.moveaxis(np.asarray(x, np.float32).astype(ml_dtypes.bfloat16).astype(np.float64), axis, -1)
    blocks = v.reshape(v.shape[:-1] + (-1, 32))
    amax = np.abs(blocks).max(-1, keepdims=True)
    byte = np.maximum(np.where(amax > 0, np.frexp(amax)[1] - 1 + 127, 0) - down, 1)
    scale = np.exp2(byte - 127.0)
    codes = (blocks / scale).astype(np.float32).astype(dtype).astype(np.float64)
    return np.moveaxis((codes * scale).reshape(v.shape), -1, axis)


WIDE = False


def mx_kscale(k):
    if not WIDE:
        return np.ones(k)
    levels = np.array([10, -10, 5, -5, 0])
    if k % 512:
        return np.exp2(np.random.permutation(np.resize(levels, k // 32))).repeat(32)
    a = np.empty((k // 512, 16))
    for p in range(k // 512):
        a[p, :8] = np.random.permutation(np.resize(levels, 8))
        for g in range(8):
            far = levels[np.abs(levels - a[p, g]) >= 10]
            a[p, g + 8] = far[np.random.randint(len(far))]
    return np.exp2(a.ravel()).repeat(32)


BF16 = ml_dtypes.bfloat16


def bf(x):
    return np.asarray(x, np.float32).astype(BF16)


def f64(x):
    return np.asarray(x).astype(np.float64)


E2M1 = np.array([0.0, 0.5, 1.0, 1.5, 2.0, 3.0, 4.0, 6.0, -0.0, -0.5, -1.0, -1.5, -2.0, -3.0, -4.0, -6.0])


def pack_weight(w, fmt):
    k, n = w.shape
    w = f64(bf(w)).reshape(k // 32, 32, n)
    amax = np.abs(w).max(1)
    if fmt == "e4m3":
        byte = np.frexp(amax)[1] - 1 + 127 - 7
    else:
        mant, ex = np.frexp(amax / 6.0)
        byte = np.where(mant > 0.5, ex, ex - 1) + 127
    byte = np.clip(np.where(amax > 0, byte, 1), 1, 254)
    scaled = (w * np.exp2(127.0 - byte)[:, None, :]).reshape(k, n).astype(np.float32)
    by_word = np.ascontiguousarray(scaled.reshape(k // 512, 128, 4, n).transpose(0, 1, 3, 2))
    if fmt == "e4m3":
        words = by_word.astype(ml_dtypes.float8_e4m3fn).view(np.uint8)
    else:
        c = by_word.astype(ml_dtypes.float4_e2m1fn).view(np.uint8) & 0xF
        words = c[..., 0::2] | (c[..., 1::2] << 4)
    return np.ascontiguousarray(words), np.ascontiguousarray(byte.astype(np.uint8).reshape(k // 512, 16, n))


def unpack_weight(words, scales, fmt):
    g, p, n, _ = words.shape
    if fmt == "e4m3":
        vals = np.ascontiguousarray(words).view(ml_dtypes.float8_e4m3fn).astype(np.float64)
    else:
        nib = np.empty((g, p, n, 4), np.uint8)
        nib[..., 0::2] = words & 0xF
        nib[..., 1::2] = words >> 4
        vals = E2M1[nib]
    vals = vals * np.repeat(np.exp2(scales.astype(np.float64) - 127.0), 8, axis=1)[..., None]
    return vals.transpose(0, 1, 3, 2).reshape(g * 512, n)
def pack4(w):
    words, scales = pack_weight(w, "e2m1")
    return words.reshape(words.shape[0], 128, -1), scales


def unpack4(words, scales):
    return unpack_weight(words.reshape(words.shape[0], 128, -1, 2), scales, "e2m1")


M, L, R, P, C = 1024, 1024, 2048, 512, 512


def setup_inputs():
    s = mx_kscale(L)
    t = mx_kscale(R)
    u = mx_kscale(M)
    conc = np.exp(1.5 * np.random.standard_normal((M, L)))
    affinity = np.exp(1.5 * np.random.standard_normal((L, R))) / L
    comp = 1 + np.exp(2 + 0.5 * np.random.standard_normal(R))
    density = np.exp(0.5 * np.random.standard_normal((M, R)))
    efficacy = np.random.standard_normal((R, P)) / np.sqrt(R)
    contrast = np.random.standard_normal((C, M)) / np.sqrt(M)
    words, scales = pack4(efficacy / t[:, None])
    return {"conc": bf(conc * s),
            "affinity": bf(affinity / s[:, None]),
            "comp": bf(comp),
            "density": bf(density * u[:, None] * t),
            "efficacy_words": words,
            "efficacy_scales": scales,
            "contrast": bf(contrast / u)}


def reference(conc, affinity, comp, density, efficacy_words, efficacy_scales, contrast):
    a = mxq(f64(conc), 1, "e4m3") @ mxq(f64(affinity), 0, "e4m3")
    b = f64(density) * (a / (a + f64(comp)))
    eff = unpack4(efficacy_words, efficacy_scales)
    response = mxq(b, 1, "e4m3") @ eff
    effect = mxq(f64(contrast), 1, "e4m3") @ mxq(b, 0, "e4m3")
    return response, effect

@@ -1,0 +1,385 @@
+from contextlib import ExitStack
+
+import concourse.mybir as mybir
+from concourse.masks import make_identity
+
+M, L, R, NP, C = 1024, 1024, 2048, 512, 512
+FLOPS = 2 * M * L * R + 2 * M * R * NP + 2 * C * M * R
+
+F32 = mybir.dt.float32
+BF16 = mybir.dt.bfloat16
+I32 = mybir.dt.int32
+U32 = mybir.dt.uint32
+U8 = mybir.dt.uint8
+FP8X4 = mybir.dt.float8_e4m3fn_x4
+FP4X4 = mybir.dt.float4_e2m1fn_x4
+ACT = mybir.ActivationFunctionType
+ALU = mybir.AluOpType
+
+P = 128
+W = 512
+TINY = 2.0 ** -60
+
+
+def tile_competitive_receptor_binding_s8_kernel(
+    tc, conc, affinity, comp, density, efficacy_words, efficacy_scales, contrast, response, effect
+):
+    nc = tc.nc
+    with ExitStack() as ctx:
+        sb = ctx.enter_context(tc.tile_pool(name="sb", bufs=1))
+        ps = ctx.enter_context(tc.psum_pool(name="ps", bufs=1))
+        ctx.enter_context(tc.manual_schedule())
+
+        def bank(k):
+            return ps.tile([P, W], F32, name="bank", tag="bank%d" % k)
+
+        def grouped():
+            return sb.tile([P, 4 * W], BF16, name="grouped", tag="grouped", bufs=5, align_bytes=64)
+
+        def big():
+            return sb.tile([P, 4, W], F32, name="big", tag="big", bufs=8, align_bytes=64)
+
+        def quantise(src, tag, bufs):
+            codes = sb.tile([P, W], U32, name="codes", tag=tag + "c", bufs=bufs, align_bytes=64)
+            scales = sb.tile([P, W], U8, name="scales", tag=tag + "s", bufs=bufs, align_bytes=64)
+            nc.vector.quantize_mx(out=codes[:].bitcast(FP8X4), scales=scales[:], in_=src[:])
+            return codes, scales
+
+        def copy_on(eng, out, in_):
+            if eng == "act":
+                nc.scalar.copy(out=out, in_=in_)
+            else:
+                nc.vector.tensor_copy(out=out, in_=in_)
+
+        ident = sb.tile([P, P], F32, name="ident")
+        eff_w = sb.tile([P, 4, 2 * NP], U8, name="eff_w", align_bytes=64)
+        eff_s = sb.tile([P, 4, NP], U8, name="eff_s", align_bytes=64)
+        comp_sb = sb.tile([P, 4, 4], BF16, name="comp_sb")
+        ln_comp = sb.tile([P, 16], F32, name="ln_comp")
+        neg_ln_comp = sb.tile([P, 16], F32, name="neg_ln_comp")
+
+        conc_raw, aff_raw, con_raw, d_raw = {}, {}, {}, {}
+        conc_g, con_g, aff_g, bm_g, br_g = {}, {}, {}, {}, {}
+        conc_q, aff_q, con_q, bm_q, br_q = {}, {}, {}, {}, {}
+        x, b, a_bank, t_bank, d_bank, o_bank, stage = {}, {}, {}, {}, {}, {}, {}
+
+        def load_conc(h, kp):
+            conc_raw[h, kp] = sb.tile([P, 4, W], BF16, name="conc_raw", tag="conc_raw", bufs=4)
+            src = conc[h * W : (h + 1) * W, kp * W : (kp + 1) * W]
+            nc.sync.dma_start(out=conc_raw[h, kp][:], in_=src.rearrange("(p j) l -> p j l", j=4))
+
+        def load_aff(g, kp):
+            aff_raw[g, kp] = sb.tile([P, 4, W], BF16, name="aff_raw", tag="raw", bufs=8)
+            src = affinity[kp * W : (kp + 1) * W, g * W : (g + 1) * W]
+            nc.sync.dma_start(out=aff_raw[g, kp][:], in_=src.rearrange("(p j) r -> p j r", j=4))
+
+        def load_con(h):
+            con_raw[h] = sb.tile([P, 4, W], BF16, name="con_raw", tag="con_raw", bufs=2)
+            src = contrast[:, h * W : (h + 1) * W]
+            nc.sync.dma_start(out=con_raw[h][:], in_=src.rearrange("(p j) m -> p j m", j=4))
+
+        def load_d(h, g):
+            d_raw[h, g] = sb.tile([P, 4, W], BF16, name="d_raw", tag="raw", bufs=8)
+            src = density[h * W : (h + 1) * W, g * W : (g + 1) * W]
+            nc.sync.dma_start(out=d_raw[h, g][:], in_=src.rearrange("(p j) r -> p j r", j=4))
+
+        def words(tile):
+            return tile[:].rearrange("p j c -> p (j c)").bitcast(F32).rearrange("p (j w) -> p j w", j=4)
+
+        def turn(dst, k, src):
+            nc.tensor.transpose(dst[:, k * P : (k + 1) * P], src, ident[:])
+
+        def t_conc(h, kp, um, k):
+            t_bank["conc", h, kp, um] = dst = bank(k)
+            w = words(conc_raw[h, kp])
+            for e in range(2):
+                for ul in range(2):
+                    turn(dst, 2 * e + ul, w[:, 2 * um + e, ul::2])
+
+        def ev_conc(h, kp, um, eng):
+            if um == 0:
+                conc_g[h, kp] = grouped()
+            out = conc_g[h, kp][:].bitcast(F32)[:, um * W : (um + 1) * W]
+            src = t_bank["conc", h, kp, um][:].rearrange("p (e u c) -> p c e u", e=2, u=2)
+            copy_on(eng, out.rearrange("p (c e u) -> p c e u", e=2, u=2), src)
+
+        def q_conc(h, kp):
+            conc_q[h, kp] = quantise(conc_g[h, kp], "conc", 4)
+
+        def il_aff(g, kp):
+            aff_g[g, kp] = grouped()
+            nc.vector.tensor_copy(
+                out=aff_g[g, kp][:].rearrange("p (t c j) -> p t c j", t=4, j=4),
+                in_=aff_raw[g, kp][:].rearrange("p j (c t) -> p t c j", t=4),
+            )
+
+        def q_aff(g, kp):
+            aff_q[g, kp] = quantise(aff_g[g, kp], "aff", 4)
+
+        def mx(out, lhs, cols, rhs_codes, rhs_scales, first, last):
+            nc.tensor.matmul_mx(
+                out=out[:],
+                lhsT=lhs[0][:, cols].bitcast(FP8X4),
+                lhsT_scale=lhs[1][:, cols],
+                rhs=rhs_codes,
+                rhs_scale=rhs_scales,
+                start=first,
+                stop=last,
+            )
+
+        def mm_a(h, g, t, kp, k):
+            if kp == 0:
+                a_bank[h, g, t] = bank(k)
+            rhs = conc_q[h, kp]
+            mx(a_bank[h, g, t], aff_q[g, kp], slice(t * P, (t + 1) * P), rhs[0][:].bitcast(FP8X4), rhs[1][:], kp == 0, kp == 1)
+
+        def ln(h, g, t):
+            if t == 0:
+                x[h, g] = big()
+            nc.scalar.activation(out=x[h, g][:, t, :], in_=a_bank[h, g, t][:], func=ACT.Ln, bias=TINY)
+
+        def t_con(h, jp, k):
+            t_bank["con", h, jp] = dst = bank(k)
+            w = words(con_raw[h])
+            for jj in range(2):
+                for um in range(2):
+                    turn(dst, 2 * jj + um, w[:, 2 * jp + jj, um::2])
+
+        def ev_con(h, jp, eng):
+            if jp == 0:
+                con_g[h] = grouped()
+            out = con_g[h][:].bitcast(F32)[:, jp * W : (jp + 1) * W]
+            src = t_bank["con", h, jp][:].rearrange("p (j u c) -> p j c u", j=2, u=2)
+            copy_on(eng, out.rearrange("p (j c u) -> p j c u", j=2, u=2), src)
+
+        def q_con(h):
+            con_q[h] = quantise(con_g[h], "con", 2)
+
+        def sig(h, g, t):
+            col = 4 * g + t
+            nc.scalar.activation(
+                out=x[h, g][:, t, :], in_=x[h, g][:, t, :], func=ACT.Sigmoid, bias=neg_ln_comp[:, col : col + 1]
+            )
+
+        def t_d(h, g, ur, k):
+            d_bank[h, g, ur] = dst = bank(k)
+            w = words(d_raw[h, g])
+            for j in range(4):
+                turn(dst, j, w[:, j, ur::2])
+
+        def mult(h, g, t):
+            if t == 0:
+                b[h, g] = sb.tile([P, 4, W], BF16, name="b", tag="b", bufs=3, align_bytes=64)
+            dens = d_bank[h, g, t // 2][:].bitcast(BF16).rearrange("p (u e c v) -> p v u c e", u=2, e=2, v=2)
+            nc.vector.tensor_tensor(
+                out=b[h, g][:, t, :].rearrange("p (u c e) -> p u c e", u=2, e=2),
+                in0=x[h, g][:, t, :].rearrange("p (u c e) -> p u c e", u=2, e=2),
+                in1=dens[:, t % 2],
+                op=ALU.mult,
+            )
+
+        def t_b(h, g, tp, k):
+            t_bank["b", h, g, tp] = dst = bank(k)
+            w = words(b[h, g])
+            for tt in range(2):
+                for um in range(2):
+                    turn(dst, 2 * tt + um, w[:, 2 * tp + tt, um * P : (um + 1) * P])
+
+        def ev_b(h, g, tp, eng):
+            if tp == 0:
+                bm_g[h, g] = grouped()
+            out = bm_g[h, g][:].bitcast(F32).rearrange("p (c s t u) -> p s c t u", s=2, t=2, u=2)
+            src = t_bank["b", h, g, tp][:].rearrange("p (t u c) -> p c t u", t=2, u=2)
+            copy_on(eng, out[:, tp], src)
+
+        def q_m(h, g):
+            bm_q[h, g] = quantise(bm_g[h, g], "bm", 4)
+
+        def il_b(h, g):
+            br_g[h, g] = grouped()
+            nc.vector.tensor_copy(
+                out=br_g[h, g][:].rearrange("p (u e c t) -> p u e c t", u=2, e=2, t=4),
+                in_=b[h, g][:].rearrange("p t (u c e) -> p u e c t", u=2, e=2),
+            )
+
+        def q_r(h, g):
+            br_q[h, g] = quantise(br_g[h, g], "br", 8)
+
+        def mm_resp(h, j, g, k):
+            if g == 0:
+                o_bank["resp", h, j] = bank(k)
+            mx(o_bank["resp", h, j], br_q[h, g], slice(j * P, (j + 1) * P), eff_w[:, g, :].bitcast(FP4X4), eff_s[:, g, :], g == 0, g == 3)
+
+        def mm_eff(g, j, h, k):
+            if h == 0:
+                o_bank["eff", g, j] = bank(k)
+            rhs = bm_q[h, g]
+            mx(o_bank["eff", g, j], con_q[h], slice(j * P, (j + 1) * P), rhs[0][:].bitcast(FP8X4), rhs[1][:], h == 0, h == 1)
+
+        def out_tile(kind, i, j, eng):
+            if j == 0:
+                stage[kind, i] = big()
+            copy_on(eng, stage[kind, i][:, j, :], o_bank[kind, i, j][:])
+            if kind == "resp":
+                dst = response[i * W : (i + 1) * W, :].rearrange("(p j) n -> p j n", j=4)
+            else:
+                dst = effect[:, i * W : (i + 1) * W].rearrange("(p j) n -> p j n", j=4)
+            nc.sync.dma_start(out=dst[:, j, :], in_=stage[kind, i][:, j, :])
+
+        nc.scalar.dma_start(out=comp_sb[:], in_=comp.rearrange("(g p t) -> p g t", g=4, t=4))
+        make_identity(nc, ident[:])
+        nc.gpsimd.memset(eff_s[:].rearrange("p g n -> p (g n)").bitcast(I32), 0)
+        load_conc(0, 0)
+        load_aff(0, 0)
+        load_conc(0, 1)
+        load_aff(0, 1)
+        load_conc(1, 0)
+        load_conc(1, 1)
+        for g in range(1, 4):
+            load_aff(g, 0)
+            load_aff(g, 1)
+        load_con(0)
+        load_con(1)
+        nc.scalar.activation(out=ln_comp[:], in_=comp_sb[:].rearrange("p g t -> p (g t)"), func=ACT.Ln)
+
+        def load_eff():
+            nc.sync.dma_start(
+                out=eff_w[:].rearrange("p g n -> p (g n)").bitcast(I32).rearrange("p (g n) -> p g n", g=4),
+                in_=efficacy_words.bitcast(I32).rearrange("g p n -> p g n"),
+            )
+            eff_s32 = eff_s[:].rearrange("p g n -> p (g n)").bitcast(I32).rearrange("p (g n) -> p g n", g=4)
+            for q in range(4):
+                nc.sync.dma_start(
+                    out=eff_s32[32 * q : 32 * q + 4],
+                    in_=efficacy_scales.bitcast(I32)[:, 4 * q : 4 * q + 4, :].rearrange("g r n -> r g n"),
+                )
+
+        chunks = [(0, 0), (1, 0), (0, 1), (1, 1), (0, 2), (0, 3), (1, 2), (1, 3)]
+
+        nc.vector.tensor_scalar(out=neg_ln_comp[:], in0=ln_comp[:], scalar1=-1.0, scalar2=None, op0=ALU.mult)
+        for um in range(2):
+            t_conc(0, 0, um, 6 + um)
+            ev_conc(0, 0, um, "act")
+        il_aff(0, 0)
+        q_conc(0, 0)
+        q_aff(0, 0)
+        for um in range(2):
+            t_conc(0, 1, um, 4 + um)
+            ev_conc(0, 1, um, "act")
+        for t in range(4):
+            mm_a(0, 0, t, 0, t)
+        il_aff(0, 1)
+        q_conc(0, 1)
+        q_aff(0, 1)
+        for um in range(2):
+            t_conc(1, 0, um, 6 + um)
+            ev_conc(1, 0, um, "act")
+        for t in range(4):
+            mm_a(0, 0, t, 1, t)
+        for um in range(2):
+            t_conc(1, 1, um, 4 + um)
+        ln(0, 0, 0)
+        ln(0, 0, 1)
+        for um in range(2):
+            ev_conc(1, 1, um, "act")
+        ln(0, 0, 2)
+        ln(0, 0, 3)
+        q_conc(1, 0)
+        il_aff(1, 0)
+        q_conc(1, 1)
+        il_aff(1, 1)
+        q_aff(1, 0)
+        q_aff(1, 1)
+        a_count = 0
+        for g in range(4):
+            for h in range(2):
+                if (h, g) != (0, 0):
+                    for t in range(4):
+                        for kp in range(2):
+                            mm_a(h, g, t, kp, (6 + a_count) % 8)
+                        ln(h, g, t)
+                        a_count += 1
+                if h == 0 and 0 < g < 3:
+                    il_aff(g + 1, 0)
+                    il_aff(g + 1, 1)
+                    q_aff(g + 1, 0)
+                    q_aff(g + 1, 1)
+        for h, g in chunks[:2]:
+            load_d(h, g)
+        load_eff()
+        for h, g in chunks[2:]:
+            load_d(h, g)
+        for hc in range(2):
+            for jp in range(2):
+                t_con(hc, jp, 2 + 2 * hc + jp)
+                ev_con(hc, jp, "dve")
+        q_con(0)
+        q_con(1)
+
+        def eff_group(ge, j, k, eng):
+            for hh in range(2):
+                mm_eff(ge, j, hh, k)
+            out_tile("eff", ge, j, eng)
+
+        for t in range(4):
+            sig(*chunks[0], t)
+        for ur in range(2):
+            t_d(*chunks[0], ur, ur)
+        for t in range(4):
+            sig(*chunks[1], t)
+        for i, (h, g) in enumerate(chunks[:7]):
+            nxt = chunks[i + 1]
+            for t in range(4):
+                mult(h, g, t)
+            for tp in range(2):
+                t_d(*nxt, tp, tp)
+                t_b(h, g, tp, 2 + tp)
+            ev_b(h, g, 0, "act")
+            if i > 0:
+                q_m(*chunks[i - 1])
+                q_r(*chunks[i - 1])
+            il_b(h, g)
+            ev_b(h, g, 1, "act")
+            if i < 6:
+                for t in range(4):
+                    sig(*chunks[i + 2], t)
+            if i in (2, 4):
+                for j in range(4):
+                    eff_group(i // 2 - 1, j, 4 + j, "act")
+            if i == 5:
+                for gg in range(3):
+                    for j in range(4):
+                        mm_resp(0, j, gg, 4 + j)
+            if i == 6:
+                for j in range(4):
+                    mm_resp(0, j, 3, 4 + j)
+                    out_tile("resp", 0, j, "act")
+                for j in range(4):
+                    for gg in range(2):
+                        mm_resp(1, j, gg, 4 + j)
+        q_m(1, 2)
+        mult(1, 3, 0)
+        mult(1, 3, 1)
+        t_b(1, 3, 0, 2)
+        ev_b(1, 3, 0, "act")
+        eff_group(2, 0, 0, "act")
+        mult(1, 3, 2)
+        mult(1, 3, 3)
+        t_b(1, 3, 1, 3)
+        ev_b(1, 3, 1, "act")
+        q_r(1, 2)
+        il_b(1, 3)
+        eff_group(2, 1, 1, "act")
+        eff_group(2, 2, 2, "act")
+        eff_group(2, 3, 0, "act")
+        for j in range(4):
+            mm_resp(1, j, 2, None)
+        q_m(1, 3)
+        q_r(1, 3)
+        eff_group(3, 0, 3, "act")
+        eff_group(3, 1, 1, "dve")
+        for j in range(4):
+            mm_resp(1, j, 3, None)
+            out_tile("resp", 1, j, "dve" if j % 2 else "act")
+        eff_group(3, 2, 2, "act")
+        eff_group(3, 3, 0, "dve")

@@ -54,13 +54,16 @@ def tile_competitive_receptor_binding_s8_kernel(
         ident = sb.tile([P, P], F32, name="ident")
         eff_w = sb.tile([P, 4, 2 * NP], U8, name="eff_w", align_bytes=64)
         eff_s = sb.tile([P, 4, NP], U8, name="eff_s", align_bytes=64)
-        comp_sb = sb.tile([P, 4, 4], BF16, name="comp_sb")
+        comp_sb = sb.tile([P, 1, 4], BF16, name="comp_sb")
+        comp_rest = sb.tile([P, 3, 4], BF16, name="comp_rest")
         ln_comp = sb.tile([P, 16], F32, name="ln_comp")
         neg_ln_comp = sb.tile([P, 16], F32, name="neg_ln_comp")
 
         conc_raw, aff_raw, con_raw, d_raw = {}, {}, {}, {}
         conc_g, con_g, aff_g, bm_g, br_g = {}, {}, {}, {}, {}
         conc_q, aff_q, con_q, bm_q, br_q = {}, {}, {}, {}, {}
+        d_sorted = {}
+        SORTED = [(0, 2), (0, 3), (1, 2), (1, 3)]
         x, b, a_bank, t_bank, d_bank, o_bank, stage = {}, {}, {}, {}, {}, {}, {}
 
         def load_conc(h, kp):
@@ -79,7 +82,10 @@ def tile_competitive_receptor_binding_s8_kernel(
             nc.sync.dma_start(out=con_raw[h][:], in_=src.rearrange("(p j) m -> p j m", j=4))
 
         def load_d(h, g):
-            d_raw[h, g] = sb.tile([P, 4, W], BF16, name="d_raw", tag="raw", bufs=8)
+            if (h, g) in SORTED:
+                d_raw[h, g] = sb.tile([P, 4, W], BF16, name="d_raw", tag="conc_raw", bufs=4)
+            else:
+                d_raw[h, g] = sb.tile([P, 4, W], BF16, name="d_raw", tag="raw", bufs=8)
             src = density[h * W : (h + 1) * W, g * W : (g + 1) * W]
             nc.sync.dma_start(out=d_raw[h, g][:], in_=src.rearrange("(p j) r -> p j r", j=4))
 
@@ -106,15 +112,16 @@ def tile_competitive_receptor_binding_s8_kernel(
         def q_conc(h, kp):
             conc_q[h, kp] = quantise(conc_g[h, kp], "conc", 4)
 
-        def il_aff(g, kp):
+        def il_aff(g, kp, eng):
             aff_g[g, kp] = grouped()
-            nc.vector.tensor_copy(
-                out=aff_g[g, kp][:].rearrange("p (t c j) -> p t c j", t=4, j=4),
-                in_=aff_raw[g, kp][:].rearrange("p j (c t) -> p t c j", t=4),
+            copy_on(
+                eng,
+                out=aff_g[g, kp][:].rearrange("p (t c i j) -> p c j i t", t=4, i=2, j=4),
+                in_=aff_raw[g, kp][:].rearrange("p j (c i t) -> p c j i t", i=2, t=4),
             )
 
         def q_aff(g, kp):
-            aff_q[g, kp] = quantise(aff_g[g, kp], "aff", 4)
+            aff_q[g, kp] = quantise(aff_g[g, kp], "aff", 6)
 
         def mx(out, lhs, cols, rhs_codes, rhs_scales, first, last):
             nc.tensor.matmul_mx(
@@ -137,6 +144,11 @@ def tile_competitive_receptor_binding_s8_kernel(
             if t == 0:
                 x[h, g] = big()
             nc.scalar.activation(out=x[h, g][:, t, :], in_=a_bank[h, g, t][:], func=ACT.Ln, bias=TINY)
+
+        def warm(k, n, src):
+            dst = bank(k)
+            for rep in range(n):
+                mx(dst, src, slice(0, P), src[0][:].bitcast(FP8X4), src[1][:], True, True)
 
         def t_con(h, jp, k):
             t_bank["con", h, jp] = dst = bank(k)
@@ -161,11 +173,17 @@ def tile_competitive_receptor_binding_s8_kernel(
                 out=x[h, g][:, t, :], in_=x[h, g][:, t, :], func=ACT.Sigmoid, bias=neg_ln_comp[:, col : col + 1]
             )
 
+        def sort_d(h, g):
+            d_sorted[h, g] = sb.tile([P, 4, 2, P], F32, name="d_sorted", tag="raw", bufs=8)
+            nc.vector.tensor_copy(out=d_sorted[h, g][:], in_=words(d_raw[h, g]).rearrange("p j (c u) -> p j u c", u=2))
+
         def t_d(h, g, ur, k):
             d_bank[h, g, ur] = dst = bank(k)
-            w = words(d_raw[h, g])
             for j in range(4):
-                turn(dst, j, w[:, j, ur::2])
+                if (h, g) in SORTED:
+                    turn(dst, j, d_sorted[h, g][:, j, ur, :])
+                else:
+                    turn(dst, j, words(d_raw[h, g])[:, j, ur::2])
 
         def mult(h, g, t):
             if t == 0:
@@ -176,6 +194,36 @@ def tile_competitive_receptor_binding_s8_kernel(
                 in0=x[h, g][:, t, :].rearrange("p (u c e) -> p u c e", u=2, e=2),
                 in1=dens[:, t % 2],
                 op=ALU.mult,
+            )
+
+        def mult_half(h, g, t, um):
+            if t == 0 and um == 0:
+                b[h, g] = sb.tile([P, 4, W], BF16, name="b", tag="b", bufs=3, align_bytes=64)
+            dens = d_bank[h, g, t // 2][:].bitcast(BF16).rearrange("p (u e c v) -> p v u c e", u=2, e=2, v=2)
+            nc.vector.tensor_tensor(
+                out=b[h, g][:, t, :].rearrange("p (u c e) -> p u c e", u=2, e=2)[:, um],
+                in0=x[h, g][:, t, :].rearrange("p (u c e) -> p u c e", u=2, e=2)[:, um],
+                in1=dens[:, t % 2, um],
+                op=ALU.mult,
+            )
+
+        def il_half(h, g, um):
+            if um == 0:
+                br_g[h, g] = grouped()
+            dst = br_g[h, g][:].rearrange("p (u e c i t) -> p u c t i e", u=2, e=2, i=2, t=4)
+            src = b[h, g][:].rearrange("p t (u c i e) -> p u c t i e", u=2, i=2, e=2)
+            nc.vector.tensor_copy(out=dst[:, um], in_=src[:, um])
+
+        def q_half(h, g, um):
+            if um == 0:
+                codes = sb.tile([P, W], U32, name="codes", tag="brc", bufs=8, align_bytes=64)
+                scales = sb.tile([P, W], U8, name="scales", tag="brs", bufs=8, align_bytes=64)
+                br_q[h, g] = codes, scales
+            cols = slice(um * 256, (um + 1) * 256)
+            nc.vector.quantize_mx(
+                out=br_q[h, g][0][:, cols].bitcast(FP8X4),
+                scales=br_q[h, g][1][:, cols],
+                in_=br_g[h, g][:, um * 1024 : (um + 1) * 1024],
             )
 
         def t_b(h, g, tp, k):
@@ -197,10 +245,19 @@ def tile_competitive_receptor_binding_s8_kernel(
 
         def il_b(h, g):
             br_g[h, g] = grouped()
-            nc.vector.tensor_copy(
-                out=br_g[h, g][:].rearrange("p (u e c t) -> p u e c t", u=2, e=2, t=4),
-                in_=b[h, g][:].rearrange("p t (u c e) -> p u e c t", u=2, e=2),
-            )
+            dst = br_g[h, g][:].rearrange("p (u e c i t) -> p u c t i e", u=2, e=2, i=2, t=4)
+            src = b[h, g][:].rearrange("p t (u c i e) -> p u c t i e", u=2, i=2, e=2)
+            for um in range(2):
+                nc.vector.tensor_copy(out=dst[:, um], in_=src[:, um])
+
+        def il_b_pool(h, g):
+            br_g[h, g] = sb.tile([P, 4 * W], BF16, name="br_pool", tag="br_pool", bufs=1, align_bytes=64)
+            dst = br_g[h, g][:].rearrange("p (j c t) -> p j c t", j=4, t=4)
+            src = b[h, g][:].rearrange("p t (u c e) -> p u e c t", u=2, e=2)
+            for j in range(4):
+                nc.gpsimd.tensor_scalar(
+                    out=dst[:, j], in0=src[:, j // 2, j % 2], scalar1=1.0, scalar2=0.0, op0=ALU.mult, op1=ALU.add
+                )
 
         def q_r(h, g):
             br_q[h, g] = quantise(br_g[h, g], "br", 8)
@@ -226,21 +283,25 @@ def tile_competitive_receptor_binding_s8_kernel(
                 dst = effect[:, i * W : (i + 1) * W].rearrange("(p j) n -> p j n", j=4)
             nc.sync.dma_start(out=dst[:, j, :], in_=stage[kind, i][:, j, :])
 
-        nc.scalar.dma_start(out=comp_sb[:], in_=comp.rearrange("(g p t) -> p g t", g=4, t=4))
+        comp_view = comp.rearrange("(g p t) -> p g t", g=4, t=4)
+        nc.scalar.dma_start(out=comp_sb[:, 0, :], in_=comp_view[:, 0, :])
         make_identity(nc, ident[:])
         nc.gpsimd.memset(eff_s[:].rearrange("p g n -> p (g n)").bitcast(I32), 0)
         load_conc(0, 0)
         load_aff(0, 0)
         load_conc(0, 1)
         load_aff(0, 1)
+        load_aff(1, 0)
+        load_aff(1, 1)
         load_conc(1, 0)
         load_conc(1, 1)
-        for g in range(1, 4):
+        for g in range(2, 4):
             load_aff(g, 0)
             load_aff(g, 1)
+        nc.sync.dma_start(out=comp_rest[:], in_=comp_view[:, 1:4, :])
         load_con(0)
         load_con(1)
-        nc.scalar.activation(out=ln_comp[:], in_=comp_sb[:].rearrange("p g t -> p (g t)"), func=ACT.Ln)
+        nc.scalar.activation(out=ln_comp[:, 0:4], in_=comp_sb[:, 0, :], func=ACT.Ln)
 
         def load_eff():
             nc.sync.dma_start(
@@ -256,130 +317,189 @@ def tile_competitive_receptor_binding_s8_kernel(
 
         chunks = [(0, 0), (1, 0), (0, 1), (1, 1), (0, 2), (0, 3), (1, 2), (1, 3)]
 
-        nc.vector.tensor_scalar(out=neg_ln_comp[:], in0=ln_comp[:], scalar1=-1.0, scalar2=None, op0=ALU.mult)
+
         for um in range(2):
             t_conc(0, 0, um, 6 + um)
             ev_conc(0, 0, um, "act")
-        il_aff(0, 0)
+
+        il_aff(0, 0, "dve")
         q_conc(0, 0)
         q_aff(0, 0)
         for um in range(2):
             t_conc(0, 1, um, 4 + um)
             ev_conc(0, 1, um, "act")
+
         for t in range(4):
             mm_a(0, 0, t, 0, t)
-        il_aff(0, 1)
+        il_aff(0, 1, "dve")
         q_conc(0, 1)
         q_aff(0, 1)
-        for um in range(2):
-            t_conc(1, 0, um, 6 + um)
-            ev_conc(1, 0, um, "act")
+        il_aff(1, 0, "act")
+        il_aff(1, 1, "dve")
+
         for t in range(4):
             mm_a(0, 0, t, 1, t)
+            ln(0, 0, t)
+        for um in range(2):
+            t_conc(1, 0, um, 6 + um)
         for um in range(2):
             t_conc(1, 1, um, 4 + um)
-        ln(0, 0, 0)
-        ln(0, 0, 1)
-        for um in range(2):
-            ev_conc(1, 1, um, "act")
-        ln(0, 0, 2)
-        ln(0, 0, 3)
-        q_conc(1, 0)
-        il_aff(1, 0)
-        q_conc(1, 1)
-        il_aff(1, 1)
         q_aff(1, 0)
         q_aff(1, 1)
+        ev_conc(1, 0, 0, "act")
+        ev_conc(1, 0, 1, "dve")
+        ev_conc(1, 1, 0, "dve")
+        q_conc(1, 0)
+        ev_conc(1, 1, 1, "dve")
+        q_conc(1, 1)
+        il_aff(2, 0, "dve")
+        il_aff(2, 1, "dve")
+        q_aff(2, 0)
+        q_aff(2, 1)
         a_count = 0
-        for g in range(4):
-            for h in range(2):
-                if (h, g) != (0, 0):
-                    for t in range(4):
-                        for kp in range(2):
-                            mm_a(h, g, t, kp, (6 + a_count) % 8)
-                        ln(h, g, t)
-                        a_count += 1
-                if h == 0 and 0 < g < 3:
-                    il_aff(g + 1, 0)
-                    il_aff(g + 1, 1)
-                    q_aff(g + 1, 0)
-                    q_aff(g + 1, 1)
-        for h, g in chunks[:2]:
+        for h, g in [(0, 1), (1, 0), (1, 1), (0, 2), (1, 2), (0, 3), (1, 3)]:
+            for t in range(4):
+                for kp in range(2):
+                    mm_a(h, g, t, kp, a_count % 8)
+                ln(h, g, t)
+                a_count += 1
+            if (h, g) == (1, 0):
+                il_aff(3, 0, "dve")
+                il_aff(3, 1, "dve")
+                q_aff(3, 0)
+                q_aff(3, 1)
+            if (h, g) == (0, 2):
+                nc.scalar.activation(out=ln_comp[:, 4:16], in_=comp_rest[:].rearrange("p g t -> p (g t)"), func=ACT.Ln)
+        for h, g in chunks[4:] + chunks[:4]:
             load_d(h, g)
         load_eff()
-        for h, g in chunks[2:]:
-            load_d(h, g)
-        for hc in range(2):
-            for jp in range(2):
-                t_con(hc, jp, 2 + 2 * hc + jp)
-                ev_con(hc, jp, "dve")
+        for h, g in chunks[4:]:
+            sort_d(h, g)
+        nc.vector.tensor_scalar(out=neg_ln_comp[:], in0=ln_comp[:], scalar1=-1.0, scalar2=None, op0=ALU.mult)
+        for jp in range(2):
+            t_con(0, jp, 4 + jp)
+            ev_con(0, jp, "dve")
+        t_d(*chunks[0], 0, 0)
+        for jp in range(2):
+            t_con(1, jp, 6 + jp)
+            ev_con(1, jp, "dve")
+        t_d(*chunks[0], 1, 1)
         q_con(0)
-        q_con(1)
+
+        pending = [(h, g, t) for h, g in chunks[2:] for t in range(4)]
+        quota = [0]
+
+        def fill(n):
+            for rep in range(min(n, len(pending), quota[0])):
+                sig(*pending.pop(0))
+                quota[0] -= 1
 
         def eff_group(ge, j, k, eng):
             for hh in range(2):
                 mm_eff(ge, j, hh, k)
             out_tile("eff", ge, j, eng)
+            fill(1)
+
+        def resp_pass(h, js, gs, eng="act"):
+            for j in js:
+                for gg in gs:
+                    mm_resp(h, j, gg, 4 + j)
+                if gs[-1] == 3:
+                    out_tile("resp", h, j, eng if eng != "both" else ("act", "dve")[j % 2])
+                    fill(1)
+
+        TM, TR = [3], [5, 6]
+
+        def mx_work(i, part):
+            if (i, part) == (2, 2):
+                for j in range(2):
+                    eff_group(0, j, 4 + j, "act")
+            if (i, part) == (3, 2):
+                for j in range(2, 4):
+                    eff_group(0, j, 4 + j, "act")
+            if (i, part) == (4, 0):
+                for j in range(2):
+                    eff_group(1, j, 4 + j, "act")
+            if (i, part) == (4, 2):
+                for j in range(2, 4):
+                    eff_group(1, j, 4 + j, "act")
+                resp_pass(0, [0, 1], [0, 1])
+            if (i, part) == (5, 0):
+                resp_pass(0, [2, 3], [0, 1])
+            if (i, part) == (5, 2):
+                resp_pass(0, [0, 1, 2, 3], [2])
+            if (i, part) == (6, 0):
+                resp_pass(0, [0, 1, 2, 3], [3])
+            if (i, part) == (6, 2):
+                resp_pass(1, [0, 1, 2, 3], [0, 1])
+            if (i, part) == (7, 0):
+                resp_pass(1, [0, 1], [2])
+                eff_group(2, 0, 2, "act")
+                eff_group(2, 1, 3, "act")
+            if (i, part) == (7, 1):
+                resp_pass(1, [2, 3], [2])
+            if (i, part) == (7, 2):
+                eff_group(2, 2, 2, "act")
+                eff_group(2, 3, 3, "act")
+                resp_pass(1, [0, 1, 2, 3], [3], "both")
+                for j in range(4):
+                    eff_group(3, j, (2, 3, 0, 1)[j], ("act", "dve")[j % 2])
 
         for t in range(4):
             sig(*chunks[0], t)
-        for ur in range(2):
-            t_d(*chunks[0], ur, ur)
         for t in range(4):
             sig(*chunks[1], t)
         for i, (h, g) in enumerate(chunks[:7]):
-            nxt = chunks[i + 1]
-            for t in range(4):
-                mult(h, g, t)
-            for tp in range(2):
-                t_d(*nxt, tp, tp)
-                t_b(h, g, tp, 2 + tp)
+            quota[0] = [6, 6, 4, 4, 0, 4, 0, 0][i]
+            mult(h, g, 0)
+            mult(h, g, 1)
+            mx_work(i, 0)
+            t_b(h, g, 0, 2 if i < 7 else 0)
+            if i < 7:
+                t_d(*chunks[i + 1], 0, 0)
             ev_b(h, g, 0, "act")
-            if i > 0:
+            mult(h, g, 2)
+            mult(h, g, 3)
+            mx_work(i, 1)
+            t_b(h, g, 1, 3 if i < 7 else 1)
+            if i < 7:
+                t_d(*chunks[i + 1], 1, 1)
+            ev_b(h, g, 1, "act")
+            if i == 0:
+                q_con(1)
+            if i > 0 and i - 1 not in TM:
                 q_m(*chunks[i - 1])
+            if i > 0 and i - 1 not in TR:
                 q_r(*chunks[i - 1])
             il_b(h, g)
-            ev_b(h, g, 1, "act")
-            if i < 6:
-                for t in range(4):
-                    sig(*chunks[i + 2], t)
-            if i in (2, 4):
-                for j in range(4):
-                    eff_group(i // 2 - 1, j, 4 + j, "act")
-            if i == 5:
-                for gg in range(3):
-                    for j in range(4):
-                        mm_resp(0, j, gg, 4 + j)
-            if i == 6:
-                for j in range(4):
-                    mm_resp(0, j, 3, 4 + j)
-                    out_tile("resp", 0, j, "act")
-                for j in range(4):
-                    for gg in range(2):
-                        mm_resp(1, j, gg, 4 + j)
+            if i in TR:
+                q_r(h, g)
+            if i in TM:
+                q_m(h, g)
+            fill(1)
+            mx_work(i, 2)
+            fill(8)
+        for t in range(4):
+            mult_half(1, 3, t, 0)
         q_m(1, 2)
-        mult(1, 3, 0)
-        mult(1, 3, 1)
-        t_b(1, 3, 0, 2)
+        il_half(1, 3, 0)
+        mult_half(1, 3, 0, 1)
+        q_half(1, 3, 0)
+        for t in range(1, 4):
+            mult_half(1, 3, t, 1)
+        resp_pass(1, [0, 1, 2, 3], [2])
+        eff_group(2, 0, 2, "act")
+        eff_group(2, 1, 3, "act")
+        resp_pass(1, [0, 1], [3])
+        t_b(1, 3, 0, 0)
+        t_b(1, 3, 1, 1)
         ev_b(1, 3, 0, "act")
-        eff_group(2, 0, 0, "act")
-        mult(1, 3, 2)
-        mult(1, 3, 3)
-        t_b(1, 3, 1, 3)
-        ev_b(1, 3, 1, "act")
-        q_r(1, 2)
-        il_b(1, 3)
-        eff_group(2, 1, 1, "act")
+        il_half(1, 3, 1)
+        ev_b(1, 3, 1, "dve")
+        q_half(1, 3, 1)
         eff_group(2, 2, 2, "act")
-        eff_group(2, 3, 0, "act")
-        for j in range(4):
-            mm_resp(1, j, 2, None)
+        eff_group(2, 3, 3, "act")
         q_m(1, 3)
-        q_r(1, 3)
-        eff_group(3, 0, 3, "act")
-        eff_group(3, 1, 1, "dve")
+        resp_pass(1, [2, 3], [3], "dve")
         for j in range(4):
-            mm_resp(1, j, 3, None)
-            out_tile("resp", 1, j, "dve" if j % 2 else "act")
-        eff_group(3, 2, 2, "act")
-        eff_group(3, 3, 0, "dve")
+            eff_group(3, j, (4, 5, 2, 3)[j], ("act", "dve")[j % 2])

@@ -3,8 +3,8 @@ from contextlib import ExitStack
 import concourse.mybir as mybir
 from concourse.masks import make_identity
 
-M, L, R, NP, C = 1024, 1024, 2048, 512, 512
-FLOPS = 2 * M * L * R + 2 * M * R * NP + 2 * C * M * R
+SAMPLES, LIGANDS, RECEPTORS, READOUTS, CONTRASTS = 1024, 1024, 2048, 512, 512
+FLOPS = 2 * SAMPLES * RECEPTORS * (LIGANDS + READOUTS + CONTRASTS)
 
 F32 = mybir.dt.float32
 BF16 = mybir.dt.bfloat16
@@ -18,488 +18,428 @@ ALU = mybir.AluOpType
 
 P = 128
 W = 512
-TINY = 2.0 ** -60
+LN_FLOOR = 2.0**-60
+
+CHUNKS = [(0, 0), (1, 0), (0, 1), (1, 1), (0, 2), (0, 3), (1, 2), (1, 3)]
+POOL_CHUNKS = 5
+BANK_TO_VECTOR_FROM = 3
+
+DENSITY_BANKS = (0, 1)
+TURNED_BANKS = (2, 3)
+SUM_BANKS = (4, 5, 6, 7)
 
 
 def tile_competitive_receptor_binding_s8_kernel(
     tc, conc, affinity, comp, density, efficacy_words, efficacy_scales, contrast, response, effect
 ):
     nc = tc.nc
+    on_vector, on_scalar = nc.vector.tensor_copy, nc.scalar.copy
     with ExitStack() as ctx:
         sb = ctx.enter_context(tc.tile_pool(name="sb", bufs=1))
         ps = ctx.enter_context(tc.psum_pool(name="ps", bufs=1))
         ctx.enter_context(tc.manual_schedule())
 
-        def bank(k):
-            return ps.tile([P, W], F32, name="bank", tag="bank%d" % k)
-
-        def grouped():
-            return sb.tile([P, 4 * W], BF16, name="grouped", tag="grouped", bufs=5, align_bytes=64)
-
-        def big():
-            return sb.tile([P, 4, W], F32, name="big", tag="big", bufs=8, align_bytes=64)
-
-        def quantise(src, tag, bufs):
-            codes = sb.tile([P, W], U32, name="codes", tag=tag + "c", bufs=bufs, align_bytes=64)
-            scales = sb.tile([P, W], U8, name="scales", tag=tag + "s", bufs=bufs, align_bytes=64)
-            nc.vector.quantize_mx(out=codes[:].bitcast(FP8X4), scales=scales[:], in_=src[:])
-            return codes, scales
-
-        def copy_on(eng, out, in_):
-            if eng == "act":
-                nc.scalar.copy(out=out, in_=in_)
-            else:
-                nc.vector.tensor_copy(out=out, in_=in_)
-
         ident = sb.tile([P, P], F32, name="ident")
-        eff_w = sb.tile([P, 4, 2 * NP], U8, name="eff_w", align_bytes=64)
-        eff_s = sb.tile([P, 4, NP], U8, name="eff_s", align_bytes=64)
-        comp_sb = sb.tile([P, 1, 4], BF16, name="comp_sb")
+        eff_words = sb.tile([P, 4, 2 * READOUTS], U8, name="eff_words", align_bytes=64)
+        eff_scales = sb.tile([P, 4, READOUTS], U8, name="eff_scales", align_bytes=64)
+        comp_first = sb.tile([P, 1, 4], BF16, name="comp_first")
         comp_rest = sb.tile([P, 3, 4], BF16, name="comp_rest")
         ln_comp = sb.tile([P, 16], F32, name="ln_comp")
         neg_ln_comp = sb.tile([P, 16], F32, name="neg_ln_comp")
 
-        conc_raw, aff_raw, con_raw, d_raw = {}, {}, {}, {}
-        conc_g, con_g, aff_g, bm_g, br_g = {}, {}, {}, {}, {}
-        conc_q, aff_q, con_q, bm_q, br_q = {}, {}, {}, {}, {}
-        d_sorted = {}
-        SORTED = [(0, 2), (0, 3), (1, 2), (1, 3)]
-        x, b, a_bank, t_bank, d_bank, o_bank, stage = {}, {}, {}, {}, {}, {}, {}
+        conc_rows, aff_rows, contrast_rows, density_rows, density_sorted = {}, {}, {}, {}, {}
+        conc_in, aff_in, contrast_in, b_sample_in, b_receptor_in = {}, {}, {}, {}, {}
+        conc_mx, aff_mx, contrast_mx, b_sample_mx, b_receptor_mx = {}, {}, {}, {}, {}
+        logit, bound, staged = {}, {}, {}
+        a_bank, turned_bank, density_bank, sum_bank = {}, {}, {}, {}
 
-        def load_conc(h, kp):
-            conc_raw[h, kp] = sb.tile([P, 4, W], BF16, name="conc_raw", tag="conc_raw", bufs=4)
-            src = conc[h * W : (h + 1) * W, kp * W : (kp + 1) * W]
-            nc.sync.dma_start(out=conc_raw[h, kp][:], in_=src.rearrange("(p j) l -> p j l", j=4))
+        def bank(k):
+            return ps.tile([P, W], F32, name="bank", tag="bank%d" % k)
 
-        def load_aff(g, kp):
-            aff_raw[g, kp] = sb.tile([P, 4, W], BF16, name="aff_raw", tag="raw", bufs=8)
-            src = affinity[kp * W : (kp + 1) * W, g * W : (g + 1) * W]
-            nc.sync.dma_start(out=aff_raw[g, kp][:], in_=src.rearrange("(p j) r -> p j r", j=4))
+        def quantise_input():
+            return sb.tile([P, 4 * W], BF16, name="mx_in", tag="mx_in", bufs=5, align_bytes=64)
 
-        def load_con(h):
-            con_raw[h] = sb.tile([P, 4, W], BF16, name="con_raw", tag="con_raw", bufs=2)
-            src = contrast[:, h * W : (h + 1) * W]
-            nc.sync.dma_start(out=con_raw[h][:], in_=src.rearrange("(p j) m -> p j m", j=4))
+        def chunk_f32():
+            return sb.tile([P, 4, W], F32, name="chunk_f32", tag="chunk_f32", bufs=8, align_bytes=64)
 
-        def load_d(h, g):
-            if (h, g) in SORTED:
-                d_raw[h, g] = sb.tile([P, 4, W], BF16, name="d_raw", tag="conc_raw", bufs=4)
-            else:
-                d_raw[h, g] = sb.tile([P, 4, W], BF16, name="d_raw", tag="raw", bufs=8)
-            src = density[h * W : (h + 1) * W, g * W : (g + 1) * W]
-            nc.sync.dma_start(out=d_raw[h, g][:], in_=src.rearrange("(p j) r -> p j r", j=4))
+        def short_lived_rows(name):
+            return sb.tile([P, 4, W], BF16, name=name, tag="short_lived", bufs=6)
 
-        def words(tile):
-            return tile[:].rearrange("p j c -> p (j c)").bitcast(F32).rearrange("p (j w) -> p j w", j=4)
+        def mx_tiles(tag, bufs):
+            codes = sb.tile([P, W], U32, name="codes", tag=tag + "_codes", bufs=bufs, align_bytes=64)
+            scales = sb.tile([P, W], U8, name="scales", tag=tag + "_scales", bufs=bufs, align_bytes=64)
+            return codes, scales
 
-        def turn(dst, k, src):
-            nc.tensor.transpose(dst[:, k * P : (k + 1) * P], src, ident[:])
+        def quantise(src, tag, bufs):
+            codes, scales = mx_tiles(tag, bufs)
+            nc.vector.quantize_mx(out=codes[:].bitcast(FP8X4), scales=scales[:], in_=src[:])
+            return codes, scales
 
-        def t_conc(h, kp, um, k):
-            t_bank["conc", h, kp, um] = dst = bank(k)
-            w = words(conc_raw[h, kp])
-            for e in range(2):
-                for ul in range(2):
-                    turn(dst, 2 * e + ul, w[:, 2 * um + e, ul::2])
+        def load_block(tile, matrix, row_block, col_block):
+            block = matrix[row_block * W : (row_block + 1) * W, col_block * W : (col_block + 1) * W]
+            nc.sync.dma_start(out=tile[:], in_=block.rearrange("(p j) n -> p j n", j=4))
 
-        def ev_conc(h, kp, um, eng):
-            if um == 0:
-                conc_g[h, kp] = grouped()
-            out = conc_g[h, kp][:].bitcast(F32)[:, um * W : (um + 1) * W]
-            src = t_bank["conc", h, kp, um][:].rearrange("p (e u c) -> p c e u", e=2, u=2)
-            copy_on(eng, out.rearrange("p (c e u) -> p c e u", e=2, u=2), src)
+        def as_i32(tile):
+            return tile[:].rearrange("p g n -> p (g n)").bitcast(I32).rearrange("p (g n) -> p g n", g=4)
 
-        def q_conc(h, kp):
-            conc_q[h, kp] = quantise(conc_g[h, kp], "conc", 4)
+        def pairs(tile):
+            return tile[:].rearrange("p j n -> p (j n)").bitcast(F32).rearrange("p (j w) -> p j w", j=4)
 
-        def il_aff(g, kp, eng):
-            aff_g[g, kp] = grouped()
-            copy_on(
-                eng,
-                out=aff_g[g, kp][:].rearrange("p (t c i j) -> p c j i t", t=4, i=2, j=4),
-                in_=aff_raw[g, kp][:].rearrange("p j (c i t) -> p c j i t", i=2, t=4),
-            )
+        def transpose(dst, quarter, src):
+            nc.tensor.transpose(dst[:, quarter * P : (quarter + 1) * P], src, ident[:])
 
-        def q_aff(g, kp):
-            aff_q[g, kp] = quantise(aff_g[g, kp], "aff", 6)
-
-        def mx(out, lhs, cols, rhs_codes, rhs_scales, first, last):
+        def mx_pass(out, stationary, j, moving_codes, moving_scales, first, last):
+            cols = slice(j * P, (j + 1) * P)
             nc.tensor.matmul_mx(
                 out=out[:],
-                lhsT=lhs[0][:, cols].bitcast(FP8X4),
-                lhsT_scale=lhs[1][:, cols],
-                rhs=rhs_codes,
-                rhs_scale=rhs_scales,
+                lhsT=stationary[0][:, cols].bitcast(FP8X4),
+                lhsT_scale=stationary[1][:, cols],
+                rhs=moving_codes,
+                rhs_scale=moving_scales,
                 start=first,
                 stop=last,
             )
 
-        def mm_a(h, g, t, kp, k):
-            if kp == 0:
+
+        def load_conc(h, lg):
+            conc_rows[h, lg] = short_lived_rows("conc_rows")
+            load_block(conc_rows[h, lg], conc, h, lg)
+
+        def load_aff(g, lg):
+            aff_rows[g, lg] = sb.tile([P, 4, W], BF16, name="aff_rows", tag="rows", bufs=8)
+            load_block(aff_rows[g, lg], affinity, lg, g)
+
+        def turn_conc(h, lg, u, k):
+            turned_bank["conc", h, lg, u] = dst = bank(k)
+            for e in range(2):
+                for v in range(2):
+                    transpose(dst, 2 * e + v, pairs(conc_rows[h, lg])[:, 2 * u + e, v::2])
+
+        def gather_conc(h, lg, u, copy):
+            if u == 0:
+                conc_in[h, lg] = quantise_input()
+            out = conc_in[h, lg][:].bitcast(F32)[:, u * W : (u + 1) * W]
+            src = turned_bank["conc", h, lg, u][:].rearrange("p (e v c) -> p c e v", e=2, v=2)
+            copy(out=out.rearrange("p (c e v) -> p c e v", e=2, v=2), in_=src)
+
+        def quantise_conc(h, lg):
+            conc_mx[h, lg] = quantise(conc_in[h, lg], "conc", 4)
+
+        def interleave_aff(g, lg, copy):
+            aff_in[g, lg] = quantise_input()
+            copy(
+                out=aff_in[g, lg][:].rearrange("p (t b i j) -> p b j i t", t=4, i=2, j=4),
+                in_=aff_rows[g, lg][:].rearrange("p j (b i t) -> p b j i t", i=2, t=4),
+            )
+
+        def quantise_aff(g, lg):
+            aff_mx[g, lg] = quantise(aff_in[g, lg], "aff", 6)
+
+        def prepare_aff(g):
+            for lg in range(2):
+                interleave_aff(g, lg, on_vector)
+            for lg in range(2):
+                quantise_aff(g, lg)
+
+        def drive_pass(h, g, t, lg, k):
+            if lg == 0:
                 a_bank[h, g, t] = bank(k)
-            rhs = conc_q[h, kp]
-            mx(a_bank[h, g, t], aff_q[g, kp], slice(t * P, (t + 1) * P), rhs[0][:].bitcast(FP8X4), rhs[1][:], kp == 0, kp == 1)
+            codes, scales = conc_mx[h, lg]
+            mx_pass(a_bank[h, g, t], aff_mx[g, lg], t, codes[:].bitcast(FP8X4), scales[:], lg == 0, lg == 1)
 
-        def ln(h, g, t):
+        def log_drive(h, g, t):
             if t == 0:
-                x[h, g] = big()
-            nc.scalar.activation(out=x[h, g][:, t, :], in_=a_bank[h, g, t][:], func=ACT.Ln, bias=TINY)
+                logit[h, g] = chunk_f32()
+            nc.scalar.activation(out=logit[h, g][:, t, :], in_=a_bank[h, g, t][:], func=ACT.Ln, bias=LN_FLOOR)
 
-        def warm(k, n, src):
-            dst = bank(k)
-            for rep in range(n):
-                mx(dst, src, slice(0, P), src[0][:].bitcast(FP8X4), src[1][:], True, True)
 
-        def t_con(h, jp, k):
-            t_bank["con", h, jp] = dst = bank(k)
-            w = words(con_raw[h])
+        def load_contrast(h):
+            contrast_rows[h] = sb.tile([P, 4, W], BF16, name="contrast_rows", tag="contrast_rows", bufs=2)
+            load_block(contrast_rows[h], contrast, 0, h)
+
+        def turn_contrast(h, jp, k):
+            turned = bank(k)
             for jj in range(2):
-                for um in range(2):
-                    turn(dst, 2 * jj + um, w[:, 2 * jp + jj, um::2])
-
-        def ev_con(h, jp, eng):
+                for u in range(2):
+                    transpose(turned, 2 * jj + u, pairs(contrast_rows[h])[:, 2 * jp + jj, u::2])
             if jp == 0:
-                con_g[h] = grouped()
-            out = con_g[h][:].bitcast(F32)[:, jp * W : (jp + 1) * W]
-            src = t_bank["con", h, jp][:].rearrange("p (j u c) -> p j c u", j=2, u=2)
-            copy_on(eng, out.rearrange("p (j c u) -> p j c u", j=2, u=2), src)
+                contrast_in[h] = quantise_input()
+            out = contrast_in[h][:].bitcast(F32)[:, jp * W : (jp + 1) * W]
+            src = turned[:].rearrange("p (j u c) -> p j c u", j=2, u=2)
+            on_vector(out=out.rearrange("p (j c u) -> p j c u", j=2, u=2), in_=src)
 
-        def q_con(h):
-            con_q[h] = quantise(con_g[h], "con", 2)
+        def quantise_contrast(h):
+            contrast_mx[h] = quantise(contrast_in[h], "contrast", 2)
 
-        def sig(h, g, t):
-            col = 4 * g + t
-            nc.scalar.activation(
-                out=x[h, g][:, t, :], in_=x[h, g][:, t, :], func=ACT.Sigmoid, bias=neg_ln_comp[:, col : col + 1]
-            )
-
-        def sort_d(h, g):
-            d_sorted[h, g] = sb.tile([P, 4, 2, P], F32, name="d_sorted", tag="raw", bufs=8)
-            nc.vector.tensor_copy(out=d_sorted[h, g][:], in_=words(d_raw[h, g]).rearrange("p j (c u) -> p j u c", u=2))
-
-        def t_d(h, g, ur, k):
-            d_bank[h, g, ur] = dst = bank(k)
-            for j in range(4):
-                if (h, g) in SORTED:
-                    turn(dst, j, d_sorted[h, g][:, j, ur, :])
-                else:
-                    turn(dst, j, words(d_raw[h, g])[:, j, ur::2])
-
-        def mult(h, g, t):
-            if t == 0:
-                b[h, g] = sb.tile([P, 4, W], BF16, name="b", tag="b", bufs=3, align_bytes=64)
-            dens = d_bank[h, g, t // 2][:].bitcast(BF16).rearrange("p (u e c v) -> p v u c e", u=2, e=2, v=2)
-            nc.vector.tensor_tensor(
-                out=b[h, g][:, t, :].rearrange("p (u c e) -> p u c e", u=2, e=2),
-                in0=x[h, g][:, t, :].rearrange("p (u c e) -> p u c e", u=2, e=2),
-                in1=dens[:, t % 2],
-                op=ALU.mult,
-            )
-
-        def mult_half(h, g, t, um):
-            if t == 0 and um == 0:
-                b[h, g] = sb.tile([P, 4, W], BF16, name="b", tag="b", bufs=3, align_bytes=64)
-            dens = d_bank[h, g, t // 2][:].bitcast(BF16).rearrange("p (u e c v) -> p v u c e", u=2, e=2, v=2)
-            nc.vector.tensor_tensor(
-                out=b[h, g][:, t, :].rearrange("p (u c e) -> p u c e", u=2, e=2)[:, um],
-                in0=x[h, g][:, t, :].rearrange("p (u c e) -> p u c e", u=2, e=2)[:, um],
-                in1=dens[:, t % 2, um],
-                op=ALU.mult,
-            )
-
-        def il_half(h, g, um):
-            if um == 0:
-                br_g[h, g] = grouped()
-            dst = br_g[h, g][:].rearrange("p (u e c i t) -> p u c t i e", u=2, e=2, i=2, t=4)
-            src = b[h, g][:].rearrange("p t (u c i e) -> p u c t i e", u=2, i=2, e=2)
-            nc.vector.tensor_copy(out=dst[:, um], in_=src[:, um])
-
-        def q_half(h, g, um):
-            if um == 0:
-                codes = sb.tile([P, W], U32, name="codes", tag="brc", bufs=8, align_bytes=64)
-                scales = sb.tile([P, W], U8, name="scales", tag="brs", bufs=8, align_bytes=64)
-                br_q[h, g] = codes, scales
-            cols = slice(um * 256, (um + 1) * 256)
-            nc.vector.quantize_mx(
-                out=br_q[h, g][0][:, cols].bitcast(FP8X4),
-                scales=br_q[h, g][1][:, cols],
-                in_=br_g[h, g][:, um * 1024 : (um + 1) * 1024],
-            )
-
-        def t_b(h, g, tp, k):
-            t_bank["b", h, g, tp] = dst = bank(k)
-            w = words(b[h, g])
-            for tt in range(2):
-                for um in range(2):
-                    turn(dst, 2 * tt + um, w[:, 2 * tp + tt, um * P : (um + 1) * P])
-
-        def ev_b(h, g, tp, eng):
-            if tp == 0:
-                bm_g[h, g] = grouped()
-            out = bm_g[h, g][:].bitcast(F32).rearrange("p (c s t u) -> p s c t u", s=2, t=2, u=2)
-            src = t_bank["b", h, g, tp][:].rearrange("p (t u c) -> p c t u", t=2, u=2)
-            copy_on(eng, out[:, tp], src)
-
-        def q_m(h, g):
-            bm_q[h, g] = quantise(bm_g[h, g], "bm", 4)
-
-        def il_b(h, g):
-            br_g[h, g] = grouped()
-            dst = br_g[h, g][:].rearrange("p (u e c i t) -> p u c t i e", u=2, e=2, i=2, t=4)
-            src = b[h, g][:].rearrange("p t (u c i e) -> p u c t i e", u=2, i=2, e=2)
-            for um in range(2):
-                nc.vector.tensor_copy(out=dst[:, um], in_=src[:, um])
-
-        def il_b_pool(h, g):
-            br_g[h, g] = sb.tile([P, 4 * W], BF16, name="br_pool", tag="br_pool", bufs=1, align_bytes=64)
-            dst = br_g[h, g][:].rearrange("p (j c t) -> p j c t", j=4, t=4)
-            src = b[h, g][:].rearrange("p t (u c e) -> p u e c t", u=2, e=2)
-            for j in range(4):
-                nc.gpsimd.tensor_scalar(
-                    out=dst[:, j], in0=src[:, j // 2, j % 2], scalar1=1.0, scalar2=0.0, op0=ALU.mult, op1=ALU.add
-                )
-
-        def q_r(h, g):
-            br_q[h, g] = quantise(br_g[h, g], "br", 8)
-
-        def mm_resp(h, j, g, k):
-            if g == 0:
-                o_bank["resp", h, j] = bank(k)
-            mx(o_bank["resp", h, j], br_q[h, g], slice(j * P, (j + 1) * P), eff_w[:, g, :].bitcast(FP4X4), eff_s[:, g, :], g == 0, g == 3)
-
-        def mm_eff(g, j, h, k):
-            if h == 0:
-                o_bank["eff", g, j] = bank(k)
-            rhs = bm_q[h, g]
-            mx(o_bank["eff", g, j], con_q[h], slice(j * P, (j + 1) * P), rhs[0][:].bitcast(FP8X4), rhs[1][:], h == 0, h == 1)
-
-        def out_tile(kind, i, j, eng):
-            if j == 0:
-                stage[kind, i] = big()
-            copy_on(eng, stage[kind, i][:, j, :], o_bank[kind, i, j][:])
-            if kind == "resp":
-                dst = response[i * W : (i + 1) * W, :].rearrange("(p j) n -> p j n", j=4)
+        def load_density(h, g):
+            if (h, g) == CHUNKS[0]:
+                density_rows[h, g] = sb.tile([P, 4, W], BF16, name="density_rows", tag="rows", bufs=8)
             else:
-                dst = effect[:, i * W : (i + 1) * W].rearrange("(p j) n -> p j n", j=4)
-            nc.sync.dma_start(out=dst[:, j, :], in_=stage[kind, i][:, j, :])
+                density_rows[h, g] = short_lived_rows("density_rows")
+            load_block(density_rows[h, g], density, h, g)
 
-        comp_view = comp.rearrange("(g p t) -> p g t", g=4, t=4)
-        nc.scalar.dma_start(out=comp_sb[:, 0, :], in_=comp_view[:, 0, :])
-        make_identity(nc, ident[:])
-        nc.gpsimd.memset(eff_s[:].rearrange("p g n -> p (g n)").bitcast(I32), 0)
-        load_conc(0, 0)
-        load_aff(0, 0)
-        load_conc(0, 1)
-        load_aff(0, 1)
-        load_aff(1, 0)
-        load_aff(1, 1)
-        load_conc(1, 0)
-        load_conc(1, 1)
-        for g in range(2, 4):
-            load_aff(g, 0)
-            load_aff(g, 1)
-        nc.sync.dma_start(out=comp_rest[:], in_=comp_view[:, 1:4, :])
-        load_con(0)
-        load_con(1)
-        nc.scalar.activation(out=ln_comp[:, 0:4], in_=comp_sb[:, 0, :], func=ACT.Ln)
+        def sort_density(h, g):
+            density_sorted[h, g] = sb.tile([P, 4, 2, P], F32, name="density_sorted", tag="rows", bufs=8)
+            on_vector(out=density_sorted[h, g][:], in_=pairs(density_rows[h, g]).rearrange("p j (c v) -> p j v c", v=2))
 
-        def load_eff():
-            nc.sync.dma_start(
-                out=eff_w[:].rearrange("p g n -> p (g n)").bitcast(I32).rearrange("p (g n) -> p g n", g=4),
-                in_=efficacy_words.bitcast(I32).rearrange("g p n -> p g n"),
-            )
-            eff_s32 = eff_s[:].rearrange("p g n -> p (g n)").bitcast(I32).rearrange("p (g n) -> p g n", g=4)
+        def load_efficacy():
+            nc.sync.dma_start(out=as_i32(eff_words), in_=efficacy_words.bitcast(I32).rearrange("g p n -> p g n"))
             for q in range(4):
                 nc.sync.dma_start(
-                    out=eff_s32[32 * q : 32 * q + 4],
+                    out=as_i32(eff_scales)[32 * q : 32 * q + 4],
                     in_=efficacy_scales.bitcast(I32)[:, 4 * q : 4 * q + 4, :].rearrange("g r n -> r g n"),
                 )
 
-        chunks = [(0, 0), (1, 0), (0, 1), (1, 1), (0, 2), (0, 3), (1, 2), (1, 3)]
 
+        def occupancy(h, g, t):
+            col = 4 * g + t
+            nc.scalar.activation(
+                out=logit[h, g][:, t, :], in_=logit[h, g][:, t, :], func=ACT.Sigmoid, bias=neg_ln_comp[:, col : col + 1]
+            )
 
-        for um in range(2):
-            t_conc(0, 0, um, 6 + um)
-            ev_conc(0, 0, um, "act")
+        def turn_density(h, g, v):
+            density_bank[h, g, v] = dst = bank(DENSITY_BANKS[v])
+            for j in range(4):
+                if (h, g) == CHUNKS[0]:
+                    transpose(dst, j, pairs(density_rows[h, g])[:, j, v::2])
+                else:
+                    transpose(dst, j, density_sorted[h, g][:, j, v, :])
 
-        il_aff(0, 0, "dve")
-        q_conc(0, 0)
-        q_aff(0, 0)
-        for um in range(2):
-            t_conc(0, 1, um, 4 + um)
-            ev_conc(0, 1, um, "act")
+        def multiply(h, g, t, us):
+            if (h, g) not in bound:
+                bound[h, g] = sb.tile([P, 4, W], BF16, name="bound", tag="bound", bufs=3, align_bytes=64)
+            dens = density_bank[h, g, t // 2][:].bitcast(BF16).rearrange("p (u e c s) -> p s u c e", u=2, e=2, s=2)
+            nc.vector.tensor_tensor(
+                out=bound[h, g][:, t, :].rearrange("p (u c e) -> p u c e", u=2, e=2)[:, us],
+                in0=logit[h, g][:, t, :].rearrange("p (u c e) -> p u c e", u=2, e=2)[:, us],
+                in1=dens[:, t % 2, us],
+                op=ALU.mult,
+            )
 
+        def turn_bound(h, g, v, k):
+            turned_bank["bound", h, g, v] = dst = bank(k)
+            for s in range(2):
+                for u in range(2):
+                    transpose(dst, 2 * s + u, pairs(bound[h, g])[:, 2 * v + s, u * P : (u + 1) * P])
+
+        def gather_bound(h, g, v, copy):
+            if v == 0:
+                b_sample_in[h, g] = quantise_input()
+            out = b_sample_in[h, g][:].bitcast(F32).rearrange("p (c v s u) -> p v c s u", v=2, s=2, u=2)
+            copy(out=out[:, v], in_=turned_bank["bound", h, g, v][:].rearrange("p (s u c) -> p c s u", s=2, u=2))
+
+        def quantise_by_sample(h, g):
+            b_sample_mx[h, g] = quantise(b_sample_in[h, g], "b_sample", 4)
+
+        def interleave_on_vector(h, g, u):
+            if u == 0:
+                b_receptor_in[h, g] = quantise_input()
+            dst = b_receptor_in[h, g][:].rearrange("p (u e b i t) -> p u b t i e", u=2, e=2, i=2, t=4)
+            src = bound[h, g][:].rearrange("p t (u b i e) -> p u b t i e", u=2, i=2, e=2)
+            on_vector(out=dst[:, u], in_=src[:, u])
+
+        def interleave_on_pool(h, g, pool_quarters):
+            b_receptor_in[h, g] = sb.tile([P, 4 * W], BF16, name="pool_out", tag="pool_out", bufs=1, align_bytes=64)
+            dst = b_receptor_in[h, g][:].rearrange("p (j c t) -> p j c t", j=4, t=4)
+            src = bound[h, g][:].rearrange("p t (u c e) -> p u e c t", u=2, e=2)
+            for j in range(4):
+                if j < pool_quarters:
+                    nc.gpsimd.tensor_scalar(
+                        out=dst[:, j], in0=src[:, j // 2, j % 2], scalar1=1.0, scalar2=0.0, op0=ALU.mult, op1=ALU.add
+                    )
+                else:
+                    on_vector(out=dst[:, j], in_=src[:, j // 2, j % 2])
+
+        def quantise_by_receptor(h, g):
+            b_receptor_mx[h, g] = quantise(b_receptor_in[h, g], "b_receptor", 8)
+
+        def quantise_half_by_receptor(h, g, u):
+            if u == 0:
+                b_receptor_mx[h, g] = mx_tiles("b_receptor", 8)
+            codes, scales = b_receptor_mx[h, g]
+            cols = slice(u * 2 * P, (u + 1) * 2 * P)
+            nc.vector.quantize_mx(
+                out=codes[:, cols].bitcast(FP8X4),
+                scales=scales[:, cols],
+                in_=b_receptor_in[h, g][:, u * 2 * W : (u + 1) * 2 * W],
+            )
+
+        def store_tile(name, block, index, j, copy):
+            if (name, index) not in staged:
+                staged[name, index] = chunk_f32()
+            copy(out=staged[name, index][:, j, :], in_=sum_bank[name, index, j][:])
+            nc.sync.dma_start(out=block.rearrange("(p j) n -> p j n", j=4)[:, j, :], in_=staged[name, index][:, j, :])
+
+        def response_passes(h, js, gs, copy=on_scalar):
+            for j in js:
+                for g in gs:
+                    if g == 0:
+                        sum_bank["response", h, j] = bank(SUM_BANKS[(j + 2 * (1 - h)) % 4])
+                    words = eff_words[:, g, :].bitcast(FP4X4)
+                    mx_pass(sum_bank["response", h, j], b_receptor_mx[h, g], j, words, eff_scales[:, g, :], g == 0, g == 3)
+                if gs[-1] == 3:
+                    store_tile("response", response[h * W : (h + 1) * W, :], h, j, copy)
+
+        def effect_tile(g, j, k, copy=on_scalar):
+            sum_bank["effect", g, j] = bank(k)
+            for h in range(2):
+                codes, scales = b_sample_mx[h, g]
+                mx_pass(sum_bank["effect", g, j], contrast_mx[h], j, codes[:].bitcast(FP8X4), scales[:], h == 0, h == 1)
+            store_tile("effect", effect[:, g * W : (g + 1) * W], g, j, copy)
+
+        def products_after(step):
+            if step in (2, 3):
+                for jj in range(2):
+                    effect_tile(0, 2 * (step - 2) + jj, SUM_BANKS[jj])
+                response_passes(0, [0, 1], [step - 2])
+            if step == 4:
+                for j in range(4):
+                    effect_tile(1, j, SUM_BANKS[j % 2])
+            if step == 5:
+                response_passes(0, [2, 3], [0, 1])
+                response_passes(0, range(4), [2])
+            if step == 6:
+                response_passes(1, range(4), [0, 1])
+
+        comp_by_partition = comp.rearrange("(g p t) -> p g t", g=4, t=4)
+        nc.scalar.dma_start(out=comp_first[:, 0, :], in_=comp_by_partition[:, 0, :])
+        make_identity(nc, ident[:])
+        nc.gpsimd.memset(eff_scales[:].rearrange("p g n -> p (g n)").bitcast(I32), 0)
+        for lg in range(2):
+            load_conc(0, lg)
+            load_aff(0, lg)
+        for lg in range(2):
+            load_aff(1, lg)
+        for lg in range(2):
+            load_conc(1, lg)
+        for g in range(2, 4):
+            for lg in range(2):
+                load_aff(g, lg)
+        nc.sync.dma_start(out=comp_rest[:], in_=comp_by_partition[:, 1:4, :])
+        nc.scalar.activation(out=ln_comp[:, 0:4], in_=comp_first[:, 0, :], func=ACT.Ln)
+
+        for u in range(2):
+            turn_conc(0, 0, u, 6 + u)
+            gather_conc(0, 0, u, on_scalar)
+        interleave_aff(0, 0, on_vector)
+        quantise_conc(0, 0)
+        quantise_aff(0, 0)
+        for u in range(2):
+            turn_conc(0, 1, u, 4 + u)
+            gather_conc(0, 1, u, on_scalar)
         for t in range(4):
-            mm_a(0, 0, t, 0, t)
-        il_aff(0, 1, "dve")
-        q_conc(0, 1)
-        q_aff(0, 1)
-        il_aff(1, 0, "act")
-        il_aff(1, 1, "dve")
-
+            drive_pass(0, 0, t, 0, t)
+        interleave_aff(0, 1, on_vector)
+        quantise_conc(0, 1)
+        quantise_aff(0, 1)
+        interleave_aff(1, 0, on_scalar)
+        interleave_aff(1, 1, on_vector)
         for t in range(4):
-            mm_a(0, 0, t, 1, t)
-            ln(0, 0, t)
-        for um in range(2):
-            t_conc(1, 0, um, 6 + um)
-        for um in range(2):
-            t_conc(1, 1, um, 4 + um)
-        q_aff(1, 0)
-        q_aff(1, 1)
-        ev_conc(1, 0, 0, "act")
-        ev_conc(1, 0, 1, "dve")
-        ev_conc(1, 1, 0, "dve")
-        q_conc(1, 0)
-        ev_conc(1, 1, 1, "dve")
-        q_conc(1, 1)
-        il_aff(2, 0, "dve")
-        il_aff(2, 1, "dve")
-        q_aff(2, 0)
-        q_aff(2, 1)
-        a_count = 0
-        for h, g in [(0, 1), (1, 0), (1, 1), (0, 2), (1, 2), (0, 3), (1, 3)]:
+            drive_pass(0, 0, t, 1, t)
+            log_drive(0, 0, t)
+        for lg in range(2):
+            for u in range(2):
+                turn_conc(1, lg, u, 6 - 2 * lg + u)
+        for lg in range(2):
+            quantise_aff(1, lg)
+        gather_conc(1, 0, 0, on_scalar)
+        gather_conc(1, 0, 1, on_vector)
+        gather_conc(1, 1, 0, on_vector)
+        quantise_conc(1, 0)
+        gather_conc(1, 1, 1, on_vector)
+        quantise_conc(1, 1)
+        prepare_aff(2)
+        for n, (h, g) in enumerate([(0, 1), (1, 0), (1, 1), (0, 2), (1, 2), (0, 3), (1, 3)]):
             for t in range(4):
-                for kp in range(2):
-                    mm_a(h, g, t, kp, a_count % 8)
-                ln(h, g, t)
-                a_count += 1
+                for lg in range(2):
+                    drive_pass(h, g, t, lg, (4 * n + t) % 8)
+                log_drive(h, g, t)
             if (h, g) == (1, 0):
-                il_aff(3, 0, "dve")
-                il_aff(3, 1, "dve")
-                q_aff(3, 0)
-                q_aff(3, 1)
+                prepare_aff(3)
             if (h, g) == (0, 2):
                 nc.scalar.activation(out=ln_comp[:, 4:16], in_=comp_rest[:].rearrange("p g t -> p (g t)"), func=ACT.Ln)
-        for h, g in chunks[4:] + chunks[:4]:
-            load_d(h, g)
-        load_eff()
-        for h, g in chunks[4:]:
-            sort_d(h, g)
+
+        for h, g in CHUNKS[1:7]:
+            load_density(h, g)
+        for h in range(2):
+            load_contrast(h)
+        load_density(*CHUNKS[0])
+        for h, g in CHUNKS[1:7]:
+            sort_density(h, g)
+        load_density(*CHUNKS[7])
+        load_efficacy()
         nc.vector.tensor_scalar(out=neg_ln_comp[:], in0=ln_comp[:], scalar1=-1.0, scalar2=None, op0=ALU.mult)
-        for jp in range(2):
-            t_con(0, jp, 4 + jp)
-            ev_con(0, jp, "dve")
-        t_d(*chunks[0], 0, 0)
-        for jp in range(2):
-            t_con(1, jp, 6 + jp)
-            ev_con(1, jp, "dve")
-        t_d(*chunks[0], 1, 1)
-        q_con(0)
+        sort_density(*CHUNKS[7])
+        for h in range(2):
+            for jp in range(2):
+                turn_contrast(h, jp, SUM_BANKS[2 * h + jp])
+            turn_density(*CHUNKS[0], h)
+        quantise_contrast(0)
 
-        pending = [(h, g, t) for h, g in chunks[2:] for t in range(4)]
-        quota = [0]
-
-        def fill(n):
-            for rep in range(min(n, len(pending), quota[0])):
-                sig(*pending.pop(0))
-                quota[0] -= 1
-
-        def eff_group(ge, j, k, eng):
-            for hh in range(2):
-                mm_eff(ge, j, hh, k)
-            out_tile("eff", ge, j, eng)
-            fill(1)
-
-        def resp_pass(h, js, gs, eng="act"):
-            for j in js:
-                for gg in gs:
-                    mm_resp(h, j, gg, 4 + j)
-                if gs[-1] == 3:
-                    out_tile("resp", h, j, eng if eng != "both" else ("act", "dve")[j % 2])
-                    fill(1)
-
-        TM, TR = [3], [5, 6]
-
-        def mx_work(i, part):
-            if (i, part) == (2, 2):
-                for j in range(2):
-                    eff_group(0, j, 4 + j, "act")
-            if (i, part) == (3, 2):
-                for j in range(2, 4):
-                    eff_group(0, j, 4 + j, "act")
-            if (i, part) == (4, 0):
-                for j in range(2):
-                    eff_group(1, j, 4 + j, "act")
-            if (i, part) == (4, 2):
-                for j in range(2, 4):
-                    eff_group(1, j, 4 + j, "act")
-                resp_pass(0, [0, 1], [0, 1])
-            if (i, part) == (5, 0):
-                resp_pass(0, [2, 3], [0, 1])
-            if (i, part) == (5, 2):
-                resp_pass(0, [0, 1, 2, 3], [2])
-            if (i, part) == (6, 0):
-                resp_pass(0, [0, 1, 2, 3], [3])
-            if (i, part) == (6, 2):
-                resp_pass(1, [0, 1, 2, 3], [0, 1])
-            if (i, part) == (7, 0):
-                resp_pass(1, [0, 1], [2])
-                eff_group(2, 0, 2, "act")
-                eff_group(2, 1, 3, "act")
-            if (i, part) == (7, 1):
-                resp_pass(1, [2, 3], [2])
-            if (i, part) == (7, 2):
-                eff_group(2, 2, 2, "act")
-                eff_group(2, 3, 3, "act")
-                resp_pass(1, [0, 1, 2, 3], [3], "both")
-                for j in range(4):
-                    eff_group(3, j, (2, 3, 0, 1)[j], ("act", "dve")[j % 2])
-
-        for t in range(4):
-            sig(*chunks[0], t)
-        for t in range(4):
-            sig(*chunks[1], t)
-        for i, (h, g) in enumerate(chunks[:7]):
-            quota[0] = [6, 6, 4, 4, 0, 4, 0, 0][i]
-            mult(h, g, 0)
-            mult(h, g, 1)
-            mx_work(i, 0)
-            t_b(h, g, 0, 2 if i < 7 else 0)
-            if i < 7:
-                t_d(*chunks[i + 1], 0, 0)
-            ev_b(h, g, 0, "act")
-            mult(h, g, 2)
-            mult(h, g, 3)
-            mx_work(i, 1)
-            t_b(h, g, 1, 3 if i < 7 else 1)
-            if i < 7:
-                t_d(*chunks[i + 1], 1, 1)
-            ev_b(h, g, 1, "act")
+        both = slice(0, 2)
+        for h, g in CHUNKS[:2]:
+            for t in range(4):
+                occupancy(h, g, t)
+        for i, (h, g) in enumerate(CHUNKS[:7]):
+            on_pool = i < POOL_CHUNKS
+            bank_to_vector = on_pool and i >= BANK_TO_VECTOR_FROM
+            multiply(h, g, 0, both)
+            multiply(h, g, 1, both)
+            if i == 6:
+                response_passes(0, [2, 3, 0, 1], [3])
+            turn_density(*CHUNKS[i + 1], 0)
+            turn_bound(h, g, 0, TURNED_BANKS[0])
+            gather_bound(h, g, 0, on_scalar)
+            multiply(h, g, 2, both)
+            multiply(h, g, 3, both)
+            turn_bound(h, g, 1, TURNED_BANKS[1])
+            turn_density(*CHUNKS[i + 1], 1)
+            if not bank_to_vector:
+                gather_bound(h, g, 1, on_scalar)
             if i == 0:
-                q_con(1)
-            if i > 0 and i - 1 not in TM:
-                q_m(*chunks[i - 1])
-            if i > 0 and i - 1 not in TR:
-                q_r(*chunks[i - 1])
-            il_b(h, g)
-            if i in TR:
-                q_r(h, g)
-            if i in TM:
-                q_m(h, g)
-            fill(1)
-            mx_work(i, 2)
-            fill(8)
+                quantise_contrast(1)
+            else:
+                quantise_by_sample(*CHUNKS[i - 1])
+            if 0 < i <= POOL_CHUNKS:
+                quantise_by_receptor(*CHUNKS[i - 1])
+            if bank_to_vector:
+                gather_bound(h, g, 1, on_vector)
+            if on_pool:
+                interleave_on_pool(h, g, 4 if bank_to_vector else 3)
+            else:
+                for u in range(2):
+                    interleave_on_vector(h, g, u)
+                quantise_by_receptor(h, g)
+            ahead = CHUNKS[i + 2 : i + 3]
+            for h2, g2 in ahead:
+                occupancy(h2, g2, 0)
+            products_after(i)
+            for h2, g2 in ahead:
+                for t in range(1, 4):
+                    occupancy(h2, g2, t)
+
+        h, g = CHUNKS[7]
         for t in range(4):
-            mult_half(1, 3, t, 0)
-        q_m(1, 2)
-        il_half(1, 3, 0)
-        mult_half(1, 3, 0, 1)
-        q_half(1, 3, 0)
+            multiply(h, g, t, 0)
+        quantise_by_sample(*CHUNKS[6])
+        interleave_on_vector(h, g, 0)
+        multiply(h, g, 0, 1)
+        quantise_half_by_receptor(h, g, 0)
         for t in range(1, 4):
-            mult_half(1, 3, t, 1)
-        resp_pass(1, [0, 1, 2, 3], [2])
-        eff_group(2, 0, 2, "act")
-        eff_group(2, 1, 3, "act")
-        resp_pass(1, [0, 1], [3])
-        t_b(1, 3, 0, 0)
-        t_b(1, 3, 1, 1)
-        ev_b(1, 3, 0, "act")
-        il_half(1, 3, 1)
-        ev_b(1, 3, 1, "dve")
-        q_half(1, 3, 1)
-        eff_group(2, 2, 2, "act")
-        eff_group(2, 3, 3, "act")
-        q_m(1, 3)
-        resp_pass(1, [2, 3], [3], "dve")
-        for j in range(4):
-            eff_group(3, j, (4, 5, 2, 3)[j], ("act", "dve")[j % 2])
+            multiply(h, g, t, 1)
+        response_passes(1, range(4), [2])
+        for j in range(2):
+            effect_tile(2, j, TURNED_BANKS[j])
+        response_passes(1, [0, 1], [3])
+        for v in range(2):
+            turn_bound(h, g, v, DENSITY_BANKS[v])
+        gather_bound(h, g, 0, on_scalar)
+        interleave_on_vector(h, g, 1)
+        gather_bound(h, g, 1, on_vector)
+        quantise_half_by_receptor(h, g, 1)
+        for j in range(2):
+            effect_tile(2, 2 + j, TURNED_BANKS[j])
+        quantise_by_sample(h, g)
+        response_passes(1, [2, 3], [3], on_vector)
+        for j, k in enumerate(SUM_BANKS[:2] + TURNED_BANKS):
+            effect_tile(3, j, k, on_vector if j % 2 else on_scalar)

@@ -21,8 +21,9 @@ W = 512
 LN_FLOOR = 2.0**-60
 
 CHUNKS = [(0, 0), (1, 0), (0, 1), (1, 1), (0, 2), (0, 3), (1, 2), (1, 3)]
-POOL_CHUNKS = 5
-BANK_TO_VECTOR_FROM = 3
+CLOSING_STEP = CHUNKS.index((0, 3)) + 1
+SORTED_FROM = 3
+SCALAR_PER_STEP = 8
 
 DENSITY_BANKS = (0, 1)
 TURNED_BANKS = (2, 3)
@@ -63,7 +64,7 @@ def tile_competitive_receptor_binding_s8_kernel(
             return sb.tile([P, 4, W], F32, name="chunk_f32", tag="chunk_f32", bufs=8, align_bytes=64)
 
         def short_lived_rows(name):
-            return sb.tile([P, 4, W], BF16, name=name, tag="short_lived", bufs=6)
+            return sb.tile([P, 4, W], BF16, name=name, tag="short_lived", bufs=8 - SORTED_FROM)
 
         def mx_tiles(tag, bufs):
             codes = sb.tile([P, W], U32, name="codes", tag=tag + "_codes", bufs=bufs, align_bytes=64)
@@ -172,10 +173,10 @@ def tile_competitive_receptor_binding_s8_kernel(
             contrast_mx[h] = quantise(contrast_in[h], "contrast", 2)
 
         def load_density(h, g):
-            if (h, g) == CHUNKS[0]:
-                density_rows[h, g] = sb.tile([P, 4, W], BF16, name="density_rows", tag="rows", bufs=8)
-            else:
+            if (h, g) in CHUNKS[SORTED_FROM:]:
                 density_rows[h, g] = short_lived_rows("density_rows")
+            else:
+                density_rows[h, g] = sb.tile([P, 4, W], BF16, name="density_rows", tag="rows", bufs=8)
             load_block(density_rows[h, g], density, h, g)
 
         def sort_density(h, g):
@@ -200,10 +201,10 @@ def tile_competitive_receptor_binding_s8_kernel(
         def turn_density(h, g, v):
             density_bank[h, g, v] = dst = bank(DENSITY_BANKS[v])
             for j in range(4):
-                if (h, g) == CHUNKS[0]:
-                    transpose(dst, j, pairs(density_rows[h, g])[:, j, v::2])
-                else:
+                if (h, g) in density_sorted:
                     transpose(dst, j, density_sorted[h, g][:, j, v, :])
+                else:
+                    transpose(dst, j, pairs(density_rows[h, g])[:, j, v::2])
 
         def multiply(h, g, t, us):
             if (h, g) not in bound:
@@ -231,24 +232,12 @@ def tile_competitive_receptor_binding_s8_kernel(
         def quantise_by_sample(h, g):
             b_sample_mx[h, g] = quantise(b_sample_in[h, g], "b_sample", 4)
 
-        def interleave_on_vector(h, g, u):
+        def interleave_bound(h, g, u):
             if u == 0:
                 b_receptor_in[h, g] = quantise_input()
             dst = b_receptor_in[h, g][:].rearrange("p (u e b i t) -> p u b t i e", u=2, e=2, i=2, t=4)
             src = bound[h, g][:].rearrange("p t (u b i e) -> p u b t i e", u=2, i=2, e=2)
             on_vector(out=dst[:, u], in_=src[:, u])
-
-        def interleave_on_pool(h, g, pool_quarters):
-            b_receptor_in[h, g] = sb.tile([P, 4 * W], BF16, name="pool_out", tag="pool_out", bufs=1, align_bytes=64)
-            dst = b_receptor_in[h, g][:].rearrange("p (j c t) -> p j c t", j=4, t=4)
-            src = bound[h, g][:].rearrange("p t (u c e) -> p u e c t", u=2, e=2)
-            for j in range(4):
-                if j < pool_quarters:
-                    nc.gpsimd.tensor_scalar(
-                        out=dst[:, j], in0=src[:, j // 2, j % 2], scalar1=1.0, scalar2=0.0, op0=ALU.mult, op1=ALU.add
-                    )
-                else:
-                    on_vector(out=dst[:, j], in_=src[:, j // 2, j % 2])
 
         def quantise_by_receptor(h, g):
             b_receptor_mx[h, g] = quantise(b_receptor_in[h, g], "b_receptor", 8)
@@ -292,14 +281,17 @@ def tile_competitive_receptor_binding_s8_kernel(
                 for jj in range(2):
                     effect_tile(0, 2 * (step - 2) + jj, SUM_BANKS[jj])
                 response_passes(0, [0, 1], [step - 2])
+                return 2
             if step == 4:
                 for j in range(4):
                     effect_tile(1, j, SUM_BANKS[j % 2])
+                return 4
             if step == 5:
                 response_passes(0, [2, 3], [0, 1])
                 response_passes(0, range(4), [2])
-            if step == 6:
+            if step == CLOSING_STEP:
                 response_passes(1, range(4), [0, 1])
+            return 0
 
         comp_by_partition = comp.rearrange("(g p t) -> p g t", g=4, t=4)
         nc.scalar.dma_start(out=comp_first[:, 0, :], in_=comp_by_partition[:, 0, :])
@@ -359,17 +351,14 @@ def tile_competitive_receptor_binding_s8_kernel(
             if (h, g) == (0, 2):
                 nc.scalar.activation(out=ln_comp[:, 4:16], in_=comp_rest[:].rearrange("p g t -> p (g t)"), func=ACT.Ln)
 
-        for h, g in CHUNKS[1:7]:
-            load_density(h, g)
         for h in range(2):
             load_contrast(h)
-        load_density(*CHUNKS[0])
-        for h, g in CHUNKS[1:7]:
-            sort_density(h, g)
-        load_density(*CHUNKS[7])
+        for h, g in CHUNKS[SORTED_FROM:] + CHUNKS[:SORTED_FROM]:
+            load_density(h, g)
         load_efficacy()
+        for h, g in CHUNKS[SORTED_FROM:]:
+            sort_density(h, g)
         nc.vector.tensor_scalar(out=neg_ln_comp[:], in0=ln_comp[:], scalar1=-1.0, scalar2=None, op0=ALU.mult)
-        sort_density(*CHUNKS[7])
         for h in range(2):
             for jp in range(2):
                 turn_contrast(h, jp, SUM_BANKS[2 * h + jp])
@@ -380,12 +369,19 @@ def tile_competitive_receptor_binding_s8_kernel(
         for h, g in CHUNKS[:2]:
             for t in range(4):
                 occupancy(h, g, t)
+        waiting = [(h, g, t) for h, g in CHUNKS[2:] for t in range(4)]
+
+        def next_occupancies(count):
+            for h, g, t in waiting[:count]:
+                occupancy(h, g, t)
+                waiting.remove((h, g, t))
+
         for i, (h, g) in enumerate(CHUNKS[:7]):
-            on_pool = i < POOL_CHUNKS
-            bank_to_vector = on_pool and i >= BANK_TO_VECTOR_FROM
             multiply(h, g, 0, both)
+            if i == CLOSING_STEP:
+                quantise_by_receptor(*CHUNKS[i - 1])
             multiply(h, g, 1, both)
-            if i == 6:
+            if i == CLOSING_STEP:
                 response_passes(0, [2, 3, 0, 1], [3])
             turn_density(*CHUNKS[i + 1], 0)
             turn_bound(h, g, 0, TURNED_BANKS[0])
@@ -394,52 +390,45 @@ def tile_competitive_receptor_binding_s8_kernel(
             multiply(h, g, 3, both)
             turn_bound(h, g, 1, TURNED_BANKS[1])
             turn_density(*CHUNKS[i + 1], 1)
-            if not bank_to_vector:
-                gather_bound(h, g, 1, on_scalar)
+            gather_bound(h, g, 1, on_scalar)
             if i == 0:
                 quantise_contrast(1)
             else:
                 quantise_by_sample(*CHUNKS[i - 1])
-            if 0 < i <= POOL_CHUNKS:
+            if 0 < i < CLOSING_STEP:
                 quantise_by_receptor(*CHUNKS[i - 1])
-            if bank_to_vector:
-                gather_bound(h, g, 1, on_vector)
-            if on_pool:
-                interleave_on_pool(h, g, 4 if bank_to_vector else 3)
-            else:
-                for u in range(2):
-                    interleave_on_vector(h, g, u)
-                quantise_by_receptor(h, g)
-            ahead = CHUNKS[i + 2 : i + 3]
-            for h2, g2 in ahead:
-                occupancy(h2, g2, 0)
-            products_after(i)
-            for h2, g2 in ahead:
-                for t in range(1, 4):
-                    occupancy(h2, g2, t)
+            for u in range(2):
+                interleave_bound(h, g, u)
+            next_occupancies(1)
+            stored = products_after(i)
+            next_occupancies(SCALAR_PER_STEP - 3 - stored)
 
         h, g = CHUNKS[7]
-        for t in range(4):
-            multiply(h, g, t, 0)
+        multiply(h, g, 0, 0)
         quantise_by_sample(*CHUNKS[6])
-        interleave_on_vector(h, g, 0)
+        for t in range(1, 4):
+            multiply(h, g, t, 0)
+        quantise_by_receptor(*CHUNKS[6])
+        interleave_bound(h, g, 0)
         multiply(h, g, 0, 1)
         quantise_half_by_receptor(h, g, 0)
         for t in range(1, 4):
             multiply(h, g, t, 1)
-        response_passes(1, range(4), [2])
         for j in range(2):
             effect_tile(2, j, TURNED_BANKS[j])
-        response_passes(1, [0, 1], [3])
-        for v in range(2):
-            turn_bound(h, g, v, DENSITY_BANKS[v])
-        gather_bound(h, g, 0, on_scalar)
-        interleave_on_vector(h, g, 1)
-        gather_bound(h, g, 1, on_vector)
-        quantise_half_by_receptor(h, g, 1)
+        response_passes(1, [0, 1], [2])
         for j in range(2):
             effect_tile(2, 2 + j, TURNED_BANKS[j])
+        response_passes(1, [0], [3])
+        for v in range(2):
+            turn_bound(h, g, v, DENSITY_BANKS[v])
+        interleave_bound(h, g, 1)
+        gather_bound(h, g, 0, on_vector)
+        gather_bound(h, g, 1, on_scalar)
+        quantise_half_by_receptor(h, g, 1)
         quantise_by_sample(h, g)
-        response_passes(1, [2, 3], [3], on_vector)
-        for j, k in enumerate(SUM_BANKS[:2] + TURNED_BANKS):
+        response_passes(1, [1], [3])
+        response_passes(1, [2], [2, 3])
+        response_passes(1, [3], [2, 3], on_vector)
+        for j, k in enumerate(TURNED_BANKS + SUM_BANKS[:2]):
             effect_tile(3, j, k, on_vector if j % 2 else on_scalar)

@@ -22,8 +22,10 @@ LN_FLOOR = 2.0**-60
 
 CHUNKS = [(0, 0), (1, 0), (0, 1), (1, 1), (0, 2), (0, 3), (1, 2), (1, 3)]
 CLOSING_STEP = CHUNKS.index((0, 3)) + 1
+BUSY_STEP = CHUNKS.index((1, 1)) + 1
 SORTED_FROM = 3
-SCALAR_PER_STEP = 8
+POOL_CHUNKS = 5
+SCALAR_PER_STEP = 7
 
 DENSITY_BANKS = (0, 1)
 TURNED_BANKS = (2, 3)
@@ -51,7 +53,7 @@ def tile_competitive_receptor_binding_s8_kernel(
         conc_rows, aff_rows, contrast_rows, density_rows, density_sorted = {}, {}, {}, {}, {}
         conc_in, aff_in, contrast_in, b_sample_in, b_receptor_in = {}, {}, {}, {}, {}
         conc_mx, aff_mx, contrast_mx, b_sample_mx, b_receptor_mx = {}, {}, {}, {}, {}
-        logit, bound, staged = {}, {}, {}
+        logit, bound, pool_half, staged = {}, {}, {}, {}
         a_bank, turned_bank, density_bank, sum_bank = {}, {}, {}, {}
 
         def bank(k):
@@ -59,6 +61,9 @@ def tile_competitive_receptor_binding_s8_kernel(
 
         def quantise_input():
             return sb.tile([P, 4 * W], BF16, name="mx_in", tag="mx_in", bufs=5, align_bytes=64)
+
+        def pool_slot(columns):
+            return sb.tile([P, columns], BF16, name="pool_slot", tag="pool_slot", bufs=1, align_bytes=64)
 
         def chunk_f32():
             return sb.tile([P, 4, W], F32, name="chunk_f32", tag="chunk_f32", bufs=8, align_bytes=64)
@@ -164,7 +169,7 @@ def tile_competitive_receptor_binding_s8_kernel(
                 for u in range(2):
                     transpose(turned, 2 * jj + u, pairs(contrast_rows[h])[:, 2 * jp + jj, u::2])
             if jp == 0:
-                contrast_in[h] = quantise_input()
+                contrast_in[h] = pool_slot(4 * W) if h == 1 else quantise_input()
             out = contrast_in[h][:].bitcast(F32)[:, jp * W : (jp + 1) * W]
             src = turned[:].rearrange("p (j u c) -> p j c u", j=2, u=2)
             on_vector(out=out.rearrange("p (j c u) -> p j c u", j=2, u=2), in_=src)
@@ -239,19 +244,32 @@ def tile_competitive_receptor_binding_s8_kernel(
             src = bound[h, g][:].rearrange("p t (u b i e) -> p u b t i e", u=2, i=2, e=2)
             on_vector(out=dst[:, u], in_=src[:, u])
 
+        def interleave_on_pool(h, g):
+            pool_half[h, g] = pool_slot(2 * W)
+            dst = pool_half[h, g][:].rearrange("p (e c t) -> p e c t", e=2, t=4)
+            src = bound[h, g][:].rearrange("p t (u c e) -> p u e c t", u=2, e=2)
+            for e in range(2):
+                nc.gpsimd.tensor_scalar(
+                    out=dst[:, e], in0=src[:, 1, e], scalar1=1.0, scalar2=0.0, op0=ALU.mult, op1=ALU.add
+                )
+
         def quantise_by_receptor(h, g):
-            b_receptor_mx[h, g] = quantise(b_receptor_in[h, g], "b_receptor", 8)
+            if (h, g) in pool_half:
+                for u in range(2):
+                    quantise_half_by_receptor(h, g, u)
+            else:
+                b_receptor_mx[h, g] = quantise(b_receptor_in[h, g], "b_receptor", 8)
 
         def quantise_half_by_receptor(h, g, u):
             if u == 0:
                 b_receptor_mx[h, g] = mx_tiles("b_receptor", 8)
             codes, scales = b_receptor_mx[h, g]
             cols = slice(u * 2 * P, (u + 1) * 2 * P)
-            nc.vector.quantize_mx(
-                out=codes[:, cols].bitcast(FP8X4),
-                scales=scales[:, cols],
-                in_=b_receptor_in[h, g][:, u * 2 * W : (u + 1) * 2 * W],
-            )
+            if u == 1 and (h, g) in pool_half:
+                src = pool_half[h, g][:]
+            else:
+                src = b_receptor_in[h, g][:, u * 2 * W : (u + 1) * 2 * W]
+            nc.vector.quantize_mx(out=codes[:, cols].bitcast(FP8X4), scales=scales[:, cols], in_=src)
 
         def store_tile(name, block, index, j, copy):
             if (name, index) not in staged:
@@ -282,7 +300,7 @@ def tile_competitive_receptor_binding_s8_kernel(
                     effect_tile(0, 2 * (step - 2) + jj, SUM_BANKS[jj])
                 response_passes(0, [0, 1], [step - 2])
                 return 2
-            if step == 4:
+            if step == BUSY_STEP:
                 for j in range(4):
                     effect_tile(1, j, SUM_BANKS[j % 2])
                 return 4
@@ -390,18 +408,25 @@ def tile_competitive_receptor_binding_s8_kernel(
             multiply(h, g, 3, both)
             turn_bound(h, g, 1, TURNED_BANKS[1])
             turn_density(*CHUNKS[i + 1], 1)
-            gather_bound(h, g, 1, on_scalar)
+            if i != BUSY_STEP:
+                gather_bound(h, g, 1, on_scalar)
             if i == 0:
                 quantise_contrast(1)
             else:
                 quantise_by_sample(*CHUNKS[i - 1])
             if 0 < i < CLOSING_STEP:
                 quantise_by_receptor(*CHUNKS[i - 1])
-            for u in range(2):
-                interleave_bound(h, g, u)
+            interleave_bound(h, g, 0)
+            if i < POOL_CHUNKS:
+                interleave_on_pool(h, g)
+            else:
+                interleave_bound(h, g, 1)
+            if i == BUSY_STEP:
+                gather_bound(h, g, 1, on_vector)
             next_occupancies(1)
             stored = products_after(i)
-            next_occupancies(SCALAR_PER_STEP - 3 - stored)
+            gathered = 1 if i == BUSY_STEP else 2
+            next_occupancies(SCALAR_PER_STEP - gathered - 1 - stored)
 
         h, g = CHUNKS[7]
         multiply(h, g, 0, 0)

from contextlib import ExitStack

import concourse.mybir as mybir
from concourse.masks import make_identity

SAMPLES, LIGANDS, RECEPTORS, READOUTS, CONTRASTS = 1024, 1024, 2048, 512, 512
FLOPS = 2 * SAMPLES * RECEPTORS * (LIGANDS + READOUTS + CONTRASTS)

F32 = mybir.dt.float32
BF16 = mybir.dt.bfloat16
I32 = mybir.dt.int32
U32 = mybir.dt.uint32
U8 = mybir.dt.uint8
FP8X4 = mybir.dt.float8_e4m3fn_x4
FP4X4 = mybir.dt.float4_e2m1fn_x4
ACT = mybir.ActivationFunctionType
ALU = mybir.AluOpType

P = 128
W = 512
LN_FLOOR = 2.0**-60

CHUNKS = [(0, 0), (1, 0), (0, 1), (1, 1), (0, 2), (0, 3), (1, 2), (1, 3)]
CLOSING_STEP = CHUNKS.index((0, 3)) + 1
BUSY_STEP = CHUNKS.index((1, 1)) + 1
SORTED_FROM = 3
POOL_CHUNKS = 5
SCALAR_PER_STEP = 7

DENSITY_BANKS = (0, 1)
TURNED_BANKS = (2, 3)
SUM_BANKS = (4, 5, 6, 7)


def tile_competitive_receptor_binding_s8_kernel(
    tc, conc, affinity, comp, density, efficacy_words, efficacy_scales, contrast, response, effect
):
    nc = tc.nc
    on_vector, on_scalar = nc.vector.tensor_copy, nc.scalar.copy
    with ExitStack() as ctx:
        sb = ctx.enter_context(tc.tile_pool(name="sb", bufs=1))
        ps = ctx.enter_context(tc.psum_pool(name="ps", bufs=1))
        ctx.enter_context(tc.manual_schedule())

        ident = sb.tile([P, P], F32, name="ident")
        eff_words = sb.tile([P, 4, 2 * READOUTS], U8, name="eff_words", align_bytes=64)
        eff_scales = sb.tile([P, 4, READOUTS], U8, name="eff_scales", align_bytes=64)
        comp_first = sb.tile([P, 1, 4], BF16, name="comp_first")
        comp_rest = sb.tile([P, 3, 4], BF16, name="comp_rest")
        ln_comp = sb.tile([P, 16], F32, name="ln_comp")
        neg_ln_comp = sb.tile([P, 16], F32, name="neg_ln_comp")

        conc_rows, aff_rows, contrast_rows, density_rows, density_sorted = {}, {}, {}, {}, {}
        conc_in, aff_in, contrast_in, b_sample_in, b_receptor_in = {}, {}, {}, {}, {}
        conc_mx, aff_mx, contrast_mx, b_sample_mx, b_receptor_mx = {}, {}, {}, {}, {}
        logit, bound, pool_half, staged = {}, {}, {}, {}
        a_bank, turned_bank, density_bank, sum_bank = {}, {}, {}, {}

        def bank(k):
            return ps.tile([P, W], F32, name="bank", tag="bank%d" % k)

        def quantise_input():
            return sb.tile([P, 4 * W], BF16, name="mx_in", tag="mx_in", bufs=5, align_bytes=64)

        def pool_slot(columns):
            return sb.tile([P, columns], BF16, name="pool_slot", tag="pool_slot", bufs=1, align_bytes=64)

        def chunk_f32():
            return sb.tile([P, 4, W], F32, name="chunk_f32", tag="chunk_f32", bufs=8, align_bytes=64)

        def short_lived_rows(name):
            return sb.tile([P, 4, W], BF16, name=name, tag="short_lived", bufs=8 - SORTED_FROM)

        def mx_tiles(tag, bufs):
            codes = sb.tile([P, W], U32, name="codes", tag=tag + "_codes", bufs=bufs, align_bytes=64)
            scales = sb.tile([P, W], U8, name="scales", tag=tag + "_scales", bufs=bufs, align_bytes=64)
            return codes, scales

        def quantise(src, tag, bufs):
            codes, scales = mx_tiles(tag, bufs)
            nc.vector.quantize_mx(out=codes[:].bitcast(FP8X4), scales=scales[:], in_=src[:])
            return codes, scales

        def load_block(tile, matrix, row_block, col_block):
            block = matrix[row_block * W : (row_block + 1) * W, col_block * W : (col_block + 1) * W]
            nc.sync.dma_start(out=tile[:], in_=block.rearrange("(p j) n -> p j n", j=4))

        def as_i32(tile):
            return tile[:].rearrange("p g n -> p (g n)").bitcast(I32).rearrange("p (g n) -> p g n", g=4)

        def pairs(tile):
            return tile[:].rearrange("p j n -> p (j n)").bitcast(F32).rearrange("p (j w) -> p j w", j=4)

        def transpose(dst, quarter, src):
            nc.tensor.transpose(dst[:, quarter * P : (quarter + 1) * P], src, ident[:])

        def mx_pass(out, stationary, j, moving_codes, moving_scales, first, last):
            cols = slice(j * P, (j + 1) * P)
            nc.tensor.matmul_mx(
                out=out[:],
                lhsT=stationary[0][:, cols].bitcast(FP8X4),
                lhsT_scale=stationary[1][:, cols],
                rhs=moving_codes,
                rhs_scale=moving_scales,
                start=first,
                stop=last,
            )


        def load_conc(h, lg):
            conc_rows[h, lg] = short_lived_rows("conc_rows")
            load_block(conc_rows[h, lg], conc, h, lg)

        def load_aff(g, lg):
            aff_rows[g, lg] = sb.tile([P, 4, W], BF16, name="aff_rows", tag="rows", bufs=8)
            load_block(aff_rows[g, lg], affinity, lg, g)

        def turn_conc(h, lg, u, k):
            turned_bank["conc", h, lg, u] = dst = bank(k)
            for e in range(2):
                for v in range(2):
                    transpose(dst, 2 * e + v, pairs(conc_rows[h, lg])[:, 2 * u + e, v::2])

        def gather_conc(h, lg, u, copy):
            if u == 0:
                conc_in[h, lg] = quantise_input()
            out = conc_in[h, lg][:].bitcast(F32)[:, u * W : (u + 1) * W]
            src = turned_bank["conc", h, lg, u][:].rearrange("p (e v c) -> p c e v", e=2, v=2)
            copy(out=out.rearrange("p (c e v) -> p c e v", e=2, v=2), in_=src)

        def quantise_conc(h, lg):
            conc_mx[h, lg] = quantise(conc_in[h, lg], "conc", 4)

        def interleave_aff(g, lg, copy):
            aff_in[g, lg] = quantise_input()
            copy(
                out=aff_in[g, lg][:].rearrange("p (t b i j) -> p b j i t", t=4, i=2, j=4),
                in_=aff_rows[g, lg][:].rearrange("p j (b i t) -> p b j i t", i=2, t=4),
            )

        def quantise_aff(g, lg):
            aff_mx[g, lg] = quantise(aff_in[g, lg], "aff", 6)

        def prepare_aff(g):
            for lg in range(2):
                interleave_aff(g, lg, on_vector)
            for lg in range(2):
                quantise_aff(g, lg)

        def drive_pass(h, g, t, lg, k):
            if lg == 0:
                a_bank[h, g, t] = bank(k)
            codes, scales = conc_mx[h, lg]
            mx_pass(a_bank[h, g, t], aff_mx[g, lg], t, codes[:].bitcast(FP8X4), scales[:], lg == 0, lg == 1)

        def log_drive(h, g, t):
            if t == 0:
                logit[h, g] = chunk_f32()
            nc.scalar.activation(out=logit[h, g][:, t, :], in_=a_bank[h, g, t][:], func=ACT.Ln, bias=LN_FLOOR)


        def load_contrast(h):
            contrast_rows[h] = sb.tile([P, 4, W], BF16, name="contrast_rows", tag="contrast_rows", bufs=2)
            load_block(contrast_rows[h], contrast, 0, h)

        def turn_contrast(h, jp, k):
            turned = bank(k)
            for jj in range(2):
                for u in range(2):
                    transpose(turned, 2 * jj + u, pairs(contrast_rows[h])[:, 2 * jp + jj, u::2])
            if jp == 0:
                contrast_in[h] = pool_slot(4 * W) if h == 1 else quantise_input()
            out = contrast_in[h][:].bitcast(F32)[:, jp * W : (jp + 1) * W]
            src = turned[:].rearrange("p (j u c) -> p j c u", j=2, u=2)
            on_vector(out=out.rearrange("p (j c u) -> p j c u", j=2, u=2), in_=src)

        def quantise_contrast(h):
            contrast_mx[h] = quantise(contrast_in[h], "contrast", 2)

        def load_density(h, g):
            if (h, g) in CHUNKS[SORTED_FROM:]:
                density_rows[h, g] = short_lived_rows("density_rows")
            else:
                density_rows[h, g] = sb.tile([P, 4, W], BF16, name="density_rows", tag="rows", bufs=8)
            load_block(density_rows[h, g], density, h, g)

        def sort_density(h, g):
            density_sorted[h, g] = sb.tile([P, 4, 2, P], F32, name="density_sorted", tag="rows", bufs=8)
            on_vector(out=density_sorted[h, g][:], in_=pairs(density_rows[h, g]).rearrange("p j (c v) -> p j v c", v=2))

        def load_efficacy():
            nc.sync.dma_start(out=as_i32(eff_words), in_=efficacy_words.bitcast(I32).rearrange("g p n -> p g n"))
            for q in range(4):
                nc.sync.dma_start(
                    out=as_i32(eff_scales)[32 * q : 32 * q + 4],
                    in_=efficacy_scales.bitcast(I32)[:, 4 * q : 4 * q + 4, :].rearrange("g r n -> r g n"),
                )


        def occupancy(h, g, t):
            col = 4 * g + t
            nc.scalar.activation(
                out=logit[h, g][:, t, :], in_=logit[h, g][:, t, :], func=ACT.Sigmoid, bias=neg_ln_comp[:, col : col + 1]
            )

        def turn_density(h, g, v):
            density_bank[h, g, v] = dst = bank(DENSITY_BANKS[v])
            for j in range(4):
                if (h, g) in density_sorted:
                    transpose(dst, j, density_sorted[h, g][:, j, v, :])
                else:
                    transpose(dst, j, pairs(density_rows[h, g])[:, j, v::2])

        def multiply(h, g, t, us):
            if (h, g) not in bound:
                bound[h, g] = sb.tile([P, 4, W], BF16, name="bound", tag="bound", bufs=3, align_bytes=64)
            dens = density_bank[h, g, t // 2][:].bitcast(BF16).rearrange("p (u e c s) -> p s u c e", u=2, e=2, s=2)
            nc.vector.tensor_tensor(
                out=bound[h, g][:, t, :].rearrange("p (u c e) -> p u c e", u=2, e=2)[:, us],
                in0=logit[h, g][:, t, :].rearrange("p (u c e) -> p u c e", u=2, e=2)[:, us],
                in1=dens[:, t % 2, us],
                op=ALU.mult,
            )

        def turn_bound(h, g, v, k):
            turned_bank["bound", h, g, v] = dst = bank(k)
            for s in range(2):
                for u in range(2):
                    transpose(dst, 2 * s + u, pairs(bound[h, g])[:, 2 * v + s, u * P : (u + 1) * P])

        def gather_bound(h, g, v, copy):
            if v == 0:
                b_sample_in[h, g] = quantise_input()
            out = b_sample_in[h, g][:].bitcast(F32).rearrange("p (c v s u) -> p v c s u", v=2, s=2, u=2)
            copy(out=out[:, v], in_=turned_bank["bound", h, g, v][:].rearrange("p (s u c) -> p c s u", s=2, u=2))

        def quantise_by_sample(h, g):
            b_sample_mx[h, g] = quantise(b_sample_in[h, g], "b_sample", 4)

        def interleave_bound(h, g, u):
            if u == 0:
                b_receptor_in[h, g] = quantise_input()
            dst = b_receptor_in[h, g][:].rearrange("p (u e b i t) -> p u b t i e", u=2, e=2, i=2, t=4)
            src = bound[h, g][:].rearrange("p t (u b i e) -> p u b t i e", u=2, i=2, e=2)
            on_vector(out=dst[:, u], in_=src[:, u])

        def interleave_on_pool(h, g):
            pool_half[h, g] = pool_slot(2 * W)
            dst = pool_half[h, g][:].rearrange("p (e c t) -> p e c t", e=2, t=4)
            src = bound[h, g][:].rearrange("p t (u c e) -> p u e c t", u=2, e=2)
            for e in range(2):
                nc.gpsimd.tensor_scalar(
                    out=dst[:, e], in0=src[:, 1, e], scalar1=1.0, scalar2=0.0, op0=ALU.mult, op1=ALU.add
                )

        def quantise_by_receptor(h, g):
            if (h, g) in pool_half:
                for u in range(2):
                    quantise_half_by_receptor(h, g, u)
            else:
                b_receptor_mx[h, g] = quantise(b_receptor_in[h, g], "b_receptor", 8)

        def quantise_half_by_receptor(h, g, u):
            if u == 0:
                b_receptor_mx[h, g] = mx_tiles("b_receptor", 8)
            codes, scales = b_receptor_mx[h, g]
            cols = slice(u * 2 * P, (u + 1) * 2 * P)
            if u == 1 and (h, g) in pool_half:
                src = pool_half[h, g][:]
            else:
                src = b_receptor_in[h, g][:, u * 2 * W : (u + 1) * 2 * W]
            nc.vector.quantize_mx(out=codes[:, cols].bitcast(FP8X4), scales=scales[:, cols], in_=src)

        def store_tile(name, block, index, j, copy):
            if (name, index) not in staged:
                staged[name, index] = chunk_f32()
            copy(out=staged[name, index][:, j, :], in_=sum_bank[name, index, j][:])
            nc.sync.dma_start(out=block.rearrange("(p j) n -> p j n", j=4)[:, j, :], in_=staged[name, index][:, j, :])

        def response_passes(h, js, gs, copy=on_scalar):
            for j in js:
                for g in gs:
                    if g == 0:
                        sum_bank["response", h, j] = bank(SUM_BANKS[(j + 2 * (1 - h)) % 4])
                    words = eff_words[:, g, :].bitcast(FP4X4)
                    mx_pass(sum_bank["response", h, j], b_receptor_mx[h, g], j, words, eff_scales[:, g, :], g == 0, g == 3)
                if gs[-1] == 3:
                    store_tile("response", response[h * W : (h + 1) * W, :], h, j, copy)

        def effect_tile(g, j, k, copy=on_scalar):
            sum_bank["effect", g, j] = bank(k)
            for h in range(2):
                codes, scales = b_sample_mx[h, g]
                mx_pass(sum_bank["effect", g, j], contrast_mx[h], j, codes[:].bitcast(FP8X4), scales[:], h == 0, h == 1)
            store_tile("effect", effect[:, g * W : (g + 1) * W], g, j, copy)

        def products_after(step):
            if step in (2, 3):
                for jj in range(2):
                    effect_tile(0, 2 * (step - 2) + jj, SUM_BANKS[jj])
                response_passes(0, [0, 1], [step - 2])
                return 2
            if step == BUSY_STEP:
                for j in range(4):
                    effect_tile(1, j, SUM_BANKS[j % 2])
                return 4
            if step == 5:
                response_passes(0, [2, 3], [0, 1])
                response_passes(0, range(4), [2])
            if step == CLOSING_STEP:
                response_passes(1, range(4), [0, 1])
            return 0

        comp_by_partition = comp.rearrange("(g p t) -> p g t", g=4, t=4)
        nc.scalar.dma_start(out=comp_first[:, 0, :], in_=comp_by_partition[:, 0, :])
        make_identity(nc, ident[:])
        nc.gpsimd.memset(eff_scales[:].rearrange("p g n -> p (g n)").bitcast(I32), 0)
        for lg in range(2):
            load_conc(0, lg)
            load_aff(0, lg)
        for lg in range(2):
            load_aff(1, lg)
        for lg in range(2):
            load_conc(1, lg)
        for g in range(2, 4):
            for lg in range(2):
                load_aff(g, lg)
        nc.sync.dma_start(out=comp_rest[:], in_=comp_by_partition[:, 1:4, :])
        nc.scalar.activation(out=ln_comp[:, 0:4], in_=comp_first[:, 0, :], func=ACT.Ln)

        for u in range(2):
            turn_conc(0, 0, u, 6 + u)
            gather_conc(0, 0, u, on_scalar)
        interleave_aff(0, 0, on_vector)
        quantise_conc(0, 0)
        quantise_aff(0, 0)
        for u in range(2):
            turn_conc(0, 1, u, 4 + u)
            gather_conc(0, 1, u, on_scalar)
        for t in range(4):
            drive_pass(0, 0, t, 0, t)
        interleave_aff(0, 1, on_vector)
        quantise_conc(0, 1)
        quantise_aff(0, 1)
        interleave_aff(1, 0, on_scalar)
        interleave_aff(1, 1, on_vector)
        for t in range(4):
            drive_pass(0, 0, t, 1, t)
            log_drive(0, 0, t)
        for lg in range(2):
            for u in range(2):
                turn_conc(1, lg, u, 6 - 2 * lg + u)
        for lg in range(2):
            quantise_aff(1, lg)
        gather_conc(1, 0, 0, on_scalar)
        gather_conc(1, 0, 1, on_vector)
        gather_conc(1, 1, 0, on_vector)
        quantise_conc(1, 0)
        gather_conc(1, 1, 1, on_vector)
        quantise_conc(1, 1)
        prepare_aff(2)
        for n, (h, g) in enumerate([(0, 1), (1, 0), (1, 1), (0, 2), (1, 2), (0, 3), (1, 3)]):
            for t in range(4):
                for lg in range(2):
                    drive_pass(h, g, t, lg, (4 * n + t) % 8)
                log_drive(h, g, t)
            if (h, g) == (1, 0):
                prepare_aff(3)
            if (h, g) == (0, 2):
                nc.scalar.activation(out=ln_comp[:, 4:16], in_=comp_rest[:].rearrange("p g t -> p (g t)"), func=ACT.Ln)

        for h in range(2):
            load_contrast(h)
        for h, g in CHUNKS[SORTED_FROM:] + CHUNKS[:SORTED_FROM]:
            load_density(h, g)
        load_efficacy()
        for h, g in CHUNKS[SORTED_FROM:]:
            sort_density(h, g)
        nc.vector.tensor_scalar(out=neg_ln_comp[:], in0=ln_comp[:], scalar1=-1.0, scalar2=None, op0=ALU.mult)
        for h in range(2):
            for jp in range(2):
                turn_contrast(h, jp, SUM_BANKS[2 * h + jp])
            turn_density(*CHUNKS[0], h)
        quantise_contrast(0)

        both = slice(0, 2)
        for h, g in CHUNKS[:2]:
            for t in range(4):
                occupancy(h, g, t)
        waiting = [(h, g, t) for h, g in CHUNKS[2:] for t in range(4)]

        def next_occupancies(count):
            for h, g, t in waiting[:count]:
                occupancy(h, g, t)
                waiting.remove((h, g, t))

        for i, (h, g) in enumerate(CHUNKS[:7]):
            multiply(h, g, 0, both)
            if i == CLOSING_STEP:
                quantise_by_receptor(*CHUNKS[i - 1])
            multiply(h, g, 1, both)
            if i == CLOSING_STEP:
                response_passes(0, [2, 3, 0, 1], [3])
            turn_density(*CHUNKS[i + 1], 0)
            turn_bound(h, g, 0, TURNED_BANKS[0])
            gather_bound(h, g, 0, on_scalar)
            multiply(h, g, 2, both)
            multiply(h, g, 3, both)
            turn_bound(h, g, 1, TURNED_BANKS[1])
            turn_density(*CHUNKS[i + 1], 1)
            if i != BUSY_STEP:
                gather_bound(h, g, 1, on_scalar)
            if i == 0:
                quantise_contrast(1)
            else:
                quantise_by_sample(*CHUNKS[i - 1])
            if 0 < i < CLOSING_STEP:
                quantise_by_receptor(*CHUNKS[i - 1])
            interleave_bound(h, g, 0)
            if i < POOL_CHUNKS:
                interleave_on_pool(h, g)
            else:
                interleave_bound(h, g, 1)
            if i == BUSY_STEP:
                gather_bound(h, g, 1, on_vector)
            next_occupancies(1)
            stored = products_after(i)
            gathered = 1 if i == BUSY_STEP else 2
            next_occupancies(SCALAR_PER_STEP - gathered - 1 - stored)

        h, g = CHUNKS[7]
        multiply(h, g, 0, 0)
        quantise_by_sample(*CHUNKS[6])
        for t in range(1, 4):
            multiply(h, g, t, 0)
        quantise_by_receptor(*CHUNKS[6])
        interleave_bound(h, g, 0)
        multiply(h, g, 0, 1)
        quantise_half_by_receptor(h, g, 0)
        for t in range(1, 4):
            multiply(h, g, t, 1)
        for j in range(2):
            effect_tile(2, j, TURNED_BANKS[j])
        response_passes(1, [0, 1], [2])
        for j in range(2):
            effect_tile(2, 2 + j, TURNED_BANKS[j])
        response_passes(1, [0], [3])
        for v in range(2):
            turn_bound(h, g, v, DENSITY_BANKS[v])
        interleave_bound(h, g, 1)
        gather_bound(h, g, 0, on_vector)
        gather_bound(h, g, 1, on_scalar)
        quantise_half_by_receptor(h, g, 1)
        quantise_by_sample(h, g)
        response_passes(1, [1], [3])
        response_passes(1, [2], [2, 3])
        response_passes(1, [3], [2, 3], on_vector)
        for j, k in enumerate(TURNED_BANKS + SUM_BANKS[:2]):
            effect_tile(3, j, k, on_vector if j % 2 else on_scalar)
